import numpy as np, ml_dtypes
CORES = [1,5,17,21,33,37,49,53]
N = 8
BF = ml_dtypes.bfloat16
V, A, S, RO = 3072, 192, 3, 3
def parts(rng):
    od = np.argsort(np.arange(V) + rng.choice(np.array([24, 400, 4 * V]), (N, 8, 1)) * rng.random((N, 8, V)), axis=-1); inv = np.argsort(od, axis=-1)
    c = rng.choice(np.array([8, 16]), (1, 8, 1, 1)); e = rng.choice(np.array([1.0, 1.5, 2.0]), (1, 8, 1, 1))
    w = np.arange(V) // c * c + (c * rng.random((N, 8, 16, V)) ** e).astype(np.int64)
    w = np.where(rng.random(w.shape) < 0.125, rng.integers(0, V, w.shape), w)
    nb = np.take_along_axis(np.take_along_axis(od[:, :, None], w, 3), inv[:, :, None], 3)
    x = np.minimum(np.maximum(rng.integers(0, 16, (1, 1, 16, V)) + rng.integers(-2, 3, (N, 8, 16, V)), 0), 15)
    return od, nb, np.take_along_axis(x, inv[:, :, None], 3)
def seeds(rng, od, m, lo, hi):
    mp = np.full((N, 8, V), V); iv = np.full((N, 8, V), V); ky = np.full((N, 8, V), 1000)
    for r in range(N):
        q = (r + 1) % N
        for g in range(8):
            h = (g + (r == N - 1)) % 8
            p = np.flatnonzero(m[r, g][od[r, g]]); w = p + 0
            e = np.flatnonzero(rng.random(len(p)) < 0.1); w[e] = p[rng.permutation(e)]
            u = od[r, g][p]; v = od[q, h][w]
            mp[r, g, u] = v; iv[q, h, v] = u; ky[q, h, v] = rng.integers(lo, hi, len(v))
    return mp, iv, ky
def pack(x, nb, mp, iv, ky):
    return {"x": np.ascontiguousarray(x.reshape(N, 128, V)).astype(np.float32).astype(BF), "nb": np.ascontiguousarray(nb.reshape(N, 128, V)).astype(np.int32),
            "mp": mp.astype(np.int32), "iv": iv.astype(np.int32), "ky": ky.astype(np.int32)}
def setup_inputs(rng):
    od, nb, x = parts(rng); m = rng.random((N, 8, V)) < rng.choice(np.array([0.35, 0.5, 0.65]), (N, 8, 1))
    return pack(x, nb, *seeds(rng, od, m, -80, 160))
def setup_inputs_room(rng):
    od, nb, x = parts(rng); m = np.ones((N, 8, V), bool); T = V // S
    for r in range(N):
        for k in range(S):
            c = np.array([A, A + 1, T, A - 1, 1, 0, A, A + 1])
            if r or k: c = rng.permutation(c)
            for g in range(8): m[r, g, k * T + rng.permutation(T)[:int(c[g])]] = False
    return pack(x, nb, *seeds(rng, od, m, -80, 300))
def setup_inputs_ties(rng):
    od, nb, x = parts(rng); m = rng.random((N, 8, V)) < 0.5
    x[:, :4] = x[:1, :1, :, :1] + 0
    x[:, 4:] = np.where(x[:, 4:, :1] < 8, 3, 4)
    mp, iv, ky = seeds(rng, od, m, 0, 1)
    ky = np.where(iv < V, rng.choice(np.array([-64, -48, -47, -33, -32, -31, -17, 999]), (N, 8, V)), 1000)
    return pack(x, nb, mp, iv, ky)
def setup_inputs_alike(rng):
    od, nb, x = parts(rng); m = rng.random((N, 8, V)) < 0.5; T = V // S
    nb[:, 0] = nb[:, 0, :1] + 0; x[:, 0] = x[:1, 0, :, :1] + 0
    m[:, 1, 0] = True; m[:, 1, V - 1] = True; nb[:, 1] = rng.choice(np.array([0, V - 1]), (N, 16, V))
    m[:, 2, 0] = False
    for r in range(N): nb[r, 2] = rng.choice(np.flatnonzero(~m[r, 2]), (16, V))
    nb[:, 3, :8] = np.arange(V)
    nb[:, 4, 1::2] = nb[:, 4, 0::2] + 0
    nb[:, 5, 8:] = nb[:, 5, :8] + 0
    few = np.array([0, 1, V // 2, V - 1]); m[:, 6, few] = True; nb[:, 6] = rng.choice(few, (N, 16, V))
    o = np.arange(V) % T; m[:, 7] = (o >= 3) & (o < T - 40)
    mp, iv, ky = seeds(rng, od, m, -80, 300)
    ky[:, 0] = np.where((iv[:, 0] < V) & (rng.random((N, V)) < 0.3), -256, ky[:, 0])
    return pack(x, nb, mp, iv, ky)
def setup_inputs_evict(rng):
    od, nb, x = parts(rng); m = rng.random((N, 8, V)) < rng.choice(np.array([0.8, 0.85, 0.9]), (N, 8, 1))
    return pack(x, nb, *seeds(rng, od, m, 209, 1000))
def setup_inputs_spread(rng):
    od, nb, x = parts(rng); m = rng.random((N, 8, V)) < rng.choice(np.array([0.05, 0.2, 0.5, 0.8, 0.95]), (N, 8, 1))
    y = (16 * rng.random((N, 8, 16, V)) ** np.exp2(rng.integers(-2, 4, (N, 8, 1, V)))).astype(np.int64)
    x = np.where(rng.random((N, 8, 1, V)) < 0.5, np.minimum(y, 15), x)
    low = (V * rng.random(nb.shape) ** 6).astype(np.int64)
    nb = np.where(rng.random(nb.shape) < rng.choice(np.array([0.02, 0.2]), (N, 8, 1, 1)), np.minimum(low, V - 1), nb)
    return pack(x, nb, *seeds(rng, od, m, -256, 1000))
def check_inputs(d):
    bad = []; x = np.asarray(d["x"]).astype(np.float32)
    if not np.all((x >= 0) & (x <= 15) & (x == np.floor(x))): bad.append("numbers of x")
    for k, lo, hi in (("nb", 0, V - 1), ("mp", 0, V), ("iv", 0, V), ("ky", -256, 1000)):
        if np.min(d[k]) < lo or np.max(d[k]) > hi: bad.append("range of " + k)
    if bad: return bad
    mp = np.asarray(d["mp"]).astype(np.int64); iv = np.asarray(d["iv"]).astype(np.int64); ky = np.asarray(d["ky"])
    r, g, u = np.nonzero(mp < V)
    if np.any(iv[(r + 1) % N, np.where(r == N - 1, g + 1, g) % 8, mp[r, g, u]] != u): bad.append("iv is not the inverse of mp")
    r, g, v = np.nonzero(iv < V)
    if np.any(mp[(r - 1) % N, np.where(r == 0, g + 7, g) % 8, iv[r, g, v]] != v): bad.append("mp is not the inverse of iv")
    if np.any((ky == 1000) != (iv == V)): bad.append("keys of unmatched nodes")
    return bad
def reference(x, nb, mp, iv, ky):
    X = x.astype(np.float32).astype(np.int64).reshape(N, 8, 16, V); B = nb.astype(np.int64).reshape(N, 8, 16, V)
    M = mp.astype(np.int64); I = iv.astype(np.int64); K = ky.astype(np.int64); T = V // S
    for t in range(RO):
        lo = (t % S) * T; todo = []
        row = ((np.arange(16) + t) & 15)[:, None]
        for r in range(N):
            q = (r + 1) % N
            for g in range(8):
                h = (g + 1) % 8 if r == N - 1 else g
                u = lo + np.flatnonzero(M[r, g, lo:lo + T] == V)[:A]
                z = M[r, g][B[r, g][:, u]]; has = z < V
                v = np.where(has, B[q, h][row, np.minimum(z, V - 1)], 0)
                s = np.add.reduce(((v[:, None] == v[None]) & has[None]).astype(np.int64), axis=1)
                d = np.add.reduce(np.abs(X[r, g][:, u][:, None] - X[q, h][:, v]), axis=0)
                sc = np.where(has & (s >= 2), d - 16 * s, 5000)
                j = np.argmin(sc, axis=0); a = np.arange(len(u)); best = sc[j, a]; v = v[j, a]
                a = np.flatnonzero(best < 5000); u, v, best = u[a], v[a], best[a]
                o = np.lexsort((u, best, v)); u, v, best = u[o], v[o], best[o]
                first = np.ones(len(v), bool); first[1:] = v[1:] != v[:-1]
                a = np.flatnonzero(first & (best < K[q, h][v])); u, v, best = u[a], v[a], best[a]
                todo.append((r, g, q, h, u, v, best, (3 * X[q, h][:, v] + X[r, g][:, u]) >> 2))
        for r, g, q, h, u, v, best, col in todo:
            old = I[q, h][v]; M[r, g, old[old < V]] = V
            M[r, g, u] = v; I[q, h, v] = u; K[q, h, v] = best; X[q, h][:, v] = col
    return {"ym": M.astype(np.float32), "yk": K.astype(np.float32)}

@@ -1,0 +1,576 @@
+from concourse.bass import DstId, RemoteDMATransfer
+from concourse.mybir import AluOpType as ALU, ActivationFunctionType as ACT
+
+V, NS, RO = 3072, 1024, 3
+SP = NS + 8
+XW = NS + 16
+D1, D2 = 3080, 3272
+TW = 3472
+OFF = 64.0
+KMAX = float(240 * 65536 + V)
+F, H, B, I, U = "float32", "float16", "bfloat16", "int32", "uint16"
+
+_S = {
+    "Min": (192, I), "Tin": (192, F), "Mt": (192, F), "Mw": (192, U), "Mq": (192, U), "sMq": (192, U),
+    "Bs": (3 * SP, I), "Bf": (3080, F), "C": (TW, F), "Bp1": (SP, I), "Bp2": (SP, I), "sB1": (SP, I), "sB2": (SP, I),
+    "X": (3280, B), "Xp1": (XW, B), "Xp2": (XW, B), "sX1": (XW, B), "sX2": (XW, B),
+    "IK": (3280, F), "Mr": (TW, F), "Ev": (3280, B), "blk": (576, I), "blf": (576, F), "blt": (192, F),
+    "Wo": (208, U), "Xo": (208, B), "W0": (208, U), "Xu0": (208, B), "sW": (208, U), "sXu": (208, B), "rf": (208, F),
+    "W1": (208, U), "Xu1": (208, B), "W2": (208, U), "Xu2": (208, B),
+    "F0": (64, B), "F12": (128, B), "S1": (80, B), "cnt": (72, F), "junk": (768, B), "cmpA": (192, B),
+    "Y16": (3072, H), "v16": (192, U), "Vh": (192, H), "Xv": (3072, B), "MX": (3072, B), "EQ": (1536, B),
+    "s2n": (192, F), "pen": (192, B), "Tk": (192, F), "Sk": (192, F),
+    "E": (384, F), "GV0": (616, F), "GV1": (616, F), "GV2": (616, F),
+    "IKg": (192, F), "rej": (192, B), "C1": (2304, B), "C2": (2304, B), "eqd": (192, B), "SZ": (192, F),
+    "Xv3": (192, B), "xr": (192, B), "xn": (192, B), "Cv": (384, F), "LR0": (408, F), "LR1": (408, F), "LR2": (408, F),
+    "DXi": (128, I), "DX": (160, F), "Gx": (128, F), "AM": (192, F), "AR": (192, F),
+    "All1": (144, B), "AllP": (144, B), "AllN": (144, B), "AllS": (144, B), "BsH": (2304, H),
+    "OB": (128, B), "OBp": (128, B), "OBm": (128, B), "OBn": (128, B), "OBh": (128, B), "tf": (128, F), "Dmi": (128, I), "Dm": (128, B),
+    "tInc": (128, B), "tExc": (128, B), "Ib": (128, B), "In": (128, B), "IW": (160, F), "I8": (128, F), "PR": (1152, H),
+    "SM": (896, B), "SMa": (896, B), "LX": (512, F), "selK": (128, B), "selI": (128, F), "rst": (192, F), "ZCf": (192, F), "ZC": (192, B),
+    "Rf": (128, F), "RfT": (128, F), "Rb": (128, B), "one": (192, B), "zro": (64, B),
+}
+_SMALL = {F: (("acc", 12), ("uwf", 12), ("v1k", 12), ("Tw", 48), ("QW", 24), ("nhi", 12), ("thr", 12), ("L", 12), ("TT", 24), ("pc", 16),
+              ("k12", 16), ("aw", 12), ("nba", 12), ("D36", 36), ("mk", 16), ("pm1", 12), ("oEf", 24)),
+          I: (("ki", 12), ("vs", 24), ("s16", 12), ("pI", 1), ("pT", 3)),
+          U: (("b16", 12), ("vw16", 12), ("o16", 36), ("m16", 72), ("prm", 12), ("us", 12), ("oE", 24))}
+_AL = {}
+for _d, _l in _SMALL.items():
+    _c = 0
+    for _n, _w in _l:
+        _AL[_n] = ("sm" + _d, _c, _w)
+        _c += (_w + 15) // 16 * 16
+    _S["sm" + _d] = (_c, _d)
+SCRATCH = {k: ("sbuf", [128, w], d) for k, (w, d) in _S.items()}
+for _k in range(8):
+    SCRATCH["P%d" % _k] = ("psum", [128, 512], F)
+
+_DS = ["d%d" % k for k in range(24)]
+_MSG = ["aMw", "aW", "aU", "aB1", "aB2", "aX1", "aX2", "aL0", "aL1", "aL2"]
+SEMAPHORES = ["qv", "qa", "qp", "qg"] + _DS + _MSG + ["l" + m for m in _MSG]
+
+
+def R(name, c0=0, c1=None, cs=1, p0=0, p1=128, ps=1):
+    if name in _AL:
+        base, o, w = _AL[name]
+        return (base, o + c0, o + (w if c1 is None else c1), cs, p0, p1, ps)
+    return (name, c0, _S[name][0] if c1 is None else c1, cs, p0, p1, ps)
+
+
+def IND(win, off):
+    return ("*", win, off)
+
+
+def _meet(a, b):
+    if a[0] not in _S:
+        return True
+    if a[3] > 1 and a[3] == b[3] and (a[1] - b[1]) % a[3]:
+        return False
+    return a[1] < b[2] and b[1] < a[2] and a[4] < b[5] and b[4] < a[5]
+
+
+def rank_program(g, core, T, topo):
+    rank = T.rank_of(core)
+    if rank is None:
+        return
+    N = len(T.cores)
+    nxt, prv = T.cores[(rank + 1) % N], T.cores[(rank - 1) % N]
+    first, last = rank == 0, rank == N - 1
+    Q = {"v": g.vector, "a": g.scalar, "p": g.tensor, "g": g, "s": g.sync}
+    count = {"v": 0, "a": 0, "p": 0, "g": 0}
+    known = {q: {} for q in Q}
+    hist = {}
+    totals = {}
+    nd = [0]
+
+    def ap(r):
+        if r[0] == "*":
+            return ap(r[1]).indirect(ap(r[2]))
+        n, c0, c1, cs, p0, p1, ps = r
+        return T[n][p0:p1:ps, c0:c1:cs] if (cs > 1 or ps > 1) else T[n][p0:p1, c0:c1]
+
+    def wait(q, sem, val, clock):
+        if known[q].get(sem, 0) < val:
+            Q[q].wait_ge(T.sem[sem], val)
+            known[q][sem] = val
+            for s, x in clock.items():
+                if known[q].get(s, 0) < x:
+                    known[q][s] = x
+
+    def order(q, reads, writes):
+        need = {}
+        for regs, w in ((reads, False), (writes, True)):
+            for r in regs:
+                psum = r[0] not in _S
+                for (r2, w2, q2, tok, clock) in hist.get(r[0], ()):
+                    if psum and q == "p" and q2 == "p":
+                        continue
+                    if (w or w2 or (psum and q != q2)) and _meet(r, r2) and need.get(tok[0], (0, None))[0] < tok[1]:
+                        need[tok[0]] = (tok[1], clock)
+        for s, (val_, clock) in sorted(need.items(), key=lambda e: -len(e[1][1])):
+            wait(q, s, val_, clock)
+
+    def note(q, reads, writes, tok):
+        clock = dict(known[q]) if q in known else {}
+        totals[tok[0]] = max(totals.get(tok[0], 0), tok[1])
+        for regs, w in ((reads, False), (writes, True)):
+            for r in regs:
+                hist.setdefault(r[0], []).append((r, w, q, tok, clock))
+
+    def op(q, out, ins, fn, more=()):
+        reads, writes = [], list(more)
+        for r in ins:
+            if isinstance(r, tuple):
+                reads += [r[1], r[2]] if r[0] == "*" else [r]
+        if out[0] == "*":
+            writes.append(out[1]); reads.append(out[2])
+        else:
+            writes.append(out)
+        order(q, reads, writes)
+        count[q] += 1
+        fn().then_inc(T.sem["q" + q], 1)
+        note(q, reads, writes, ("q" + q, count[q]))
+
+    def val(x):
+        return ap(x) if isinstance(x, tuple) else x
+
+    def cp(out, in_):
+        op("v", out, [in_], lambda: g.vector.tensor_copy(ap(out), ap(in_)))
+
+    def tt(out, a, b, o):
+        op("v", out, [a, b], lambda: g.vector.tensor_tensor(ap(out), ap(a), ap(b), o))
+
+    def ts(out, a, s1, o0, s2=None, o1=None):
+        if o1 is None:
+            op("v", out, [a, s1], lambda: g.vector.tensor_scalar(ap(out), ap(a), val(s1), None, o0))
+        else:
+            op("v", out, [a, s1, s2], lambda: g.vector.tensor_scalar(ap(out), ap(a), val(s1), val(s2), o0, o1))
+
+    def scan(out, d0, d1, init, o0, o1):
+        op("v", out, [d0, d1], lambda: g.vector.tensor_tensor_scan(ap(out), ap(d0), ap(d1), init, o0, o1))
+
+    def tr(out, in_):
+        op("v", out, [in_], lambda: g.vector.transpose(ap(out), ap(in_)))
+
+    def ms(out, c):
+        op("v", out, [], lambda: g.vector.memset(ap(out), c))
+
+    def act(out, in_, f, bias=0.0, scale=1.0, acc=None):
+        if out[0] == "*":
+            op("a", out, [in_], lambda: g.scalar.activation(ap(out), ap(in_), f))
+        elif acc is None:
+            op("a", out, [in_, bias, scale], lambda: g.scalar.activation(ap(out), ap(in_), f, bias=val(bias), scale=val(scale)))
+        else:
+            op("a", out, [in_, bias, scale], lambda: g.scalar.activation(ap(out), ap(in_), f, bias=val(bias), scale=val(scale), accum_out=ap(acc)), [acc])
+
+    def mm(out, lhsT, rhs, start, stop):
+        op("p", out, [lhsT, rhs], lambda: g.tensor.matmul(ap(out), ap(lhsT), ap(rhs), start, stop))
+
+    def iota(out, pattern, base, cm):
+        if _S[out[0]][1] == I:
+            op("g", out, [], lambda: g.iota(ap(out), pattern, base, cm))
+        else:
+            op("g", out, [], lambda: g.iota(ap(out), pattern, base, cm, allow_small_or_imprecise_dtypes=True))
+
+    def select(out, in_, pattern, cmp, base, cm, fill=0.0):
+        op("g", out, [in_], lambda: g.affine_select(ap(out), ap(in_), pattern, cmp, fill, base, cm))
+
+    def dma(q, pairs):
+        sem = _DS[nd[0]]; nd[0] += 1
+        reads = [s for d, s in pairs if isinstance(s, tuple)]
+        writes = [d for d, s in pairs if isinstance(d, tuple)]
+        order(q, reads, writes)
+        for d, s in pairs:
+            Q[q].dma_start(val(d), val(s)).then_inc(T.sem[sem], 16)
+        note(q, reads, writes, (sem, 16 * len(pairs)))
+
+    def engs(src, dst):
+        return topo.engines(src, dst)[:8]
+
+    def send(msg, dst, there, here):
+        order("g", [here], [])
+        rid, pid = topo.addr(dst)[:2]
+        es = engs(core, dst)
+        g.remote_dma(ap(there), ap(here), T.sem[msg], T.sem["l" + msg], pid, rid, sum(1 << e for e in es))
+        note("g", [here], [], ("l" + msg, len(es)))
+
+    def land(final, stage, at_first):
+        return R(stage) if at_first else R(final)
+
+    def turn(final, stage):
+        if first:
+            dma("s", [(R(final, p0=16, p1=128), R(stage, p0=0, p1=112)), (R(final, p0=0, p1=16), R(stage, p0=112, p1=128))])
+
+    def turn_lists(final, stage, n, between=lambda: None):
+        if first:
+            cp(R("rf", 0, n), R(stage, 0, n))
+            mm(P(7, 0, n), R("Rf"), R("rf", 0, n), True, True)
+        between()
+        if first:
+            cp(R(final, 0, n), P(7, 0, n))
+
+    for m, f, s in (("aMw", "Mq", "sMq"), ("aW", "W0", "sW"), ("aU", "Xu0", "sXu"), ("aB1", "Bp1", "sB1"), ("aB2", "Bp2", "sB2"),
+                    ("aX1", "Xp1", "sX1"), ("aX2", "Xp2", "sX2")):
+        note("x", [], [land(f, s, first)], (m, len(engs(prv, core))))
+    for t in range(RO):
+        note("x", [], [R("LR%d" % t, 192, 408)], ("aL%d" % t, len(engs(nxt, core))))
+
+    eq, add, mul, mx, mn = ALU.is_equal, ALU.add, ALU.mult, ALU.max, ALU.min
+    ID, CP = ACT.Identity, ACT.Copy
+    col = lambda n, c: R(n, c, c + 1)
+    P = lambda k, c0, c1, cs=1: ("P%d" % k, c0, c1, cs, 0, 128, 1)
+    sel = lambda n, j, i=0: R(n, 144 * i + 15 - j, 144 * i + 143 - j)
+    PM, PG, H1, P15, H0, CJ, NPM, CG, CT, CE = (col("pc", k) for k in range(10))
+    If = R("IW", 16, 144)
+
+    dma("s", [(R("Min", 96 * h, 96 * h + 96), T.mp[h::2, :]) for h in range(2)])
+    dma("s", [(R("Bs", 0, NS), T.nb[:, 0:NS])])
+    dma("s", [(R("Bs", SP, SP + NS), T.nb[:, NS:2 * NS])])
+    dma("s", [(R("Bs", 2 * SP, 2 * SP + 512), T.nb[:, 2 * NS:2 * NS + 512])])
+    dma("s", [(R("Bs", 2 * SP + 512, 2 * SP + NS), T.nb[:, 2 * NS + 512:3 * NS])])
+    dma("s", [(R("X", 0, V), T.x[:, :])])
+    dma("s", [(R("blk", 0, 192), T.mp[:, :]), (R("blk", 192, 384), T.ky[:, :]), (R("blk", 384, 576), T.iv[:, :])])
+
+    iota(R("pI"), [[0, 1]], 0, 1)
+    iota(R("pm1"), [[16, 6], [96, 2]], 0, 0)
+    iota(R("Gx"), [[1, 8], [0, 16]], 0, 0)
+    iota(R("k12"), [[1, 16]], 0, 0)
+    iota(R("DX"), [[-1, 160]], 0, 1)
+    ms(R("zro"), 0.0)
+    ms(R("S1", 0, 8), 0.0)
+    ms(R("cnt", 64, 72), 30000.0)
+    ts(col("pT", 0), R("pI"), 15, ALU.bitwise_and)
+    ts(col("pT", 1), R("pI"), 4, ALU.arith_shift_right)
+    ts(col("pT", 2), R("pI"), 4, ALU.arith_shift_right, 1, ALU.bitwise_and)
+    for k in range(3):
+        ms(R("Bs", k * SP + NS, k * SP + SP), V)
+    cp(R("pc", 0, 3), R("pT"))
+    ms(R("Wo", 204, 208), 0); ms(R("Xo", 192, 208), 0.0)
+    ts(R("prm"), R("pm1"), PM, add)
+    ts(R("OB"), R("Gx"), PG, eq)
+    ts(P15, PM, -15.0, add)
+    ts(R("aw"), R("k12", 0, 12), 16.0, mul, PM, add)
+    ts(R("mk"), R("k12"), PM, eq)
+    select(R("tInc"), R("OB"), [[1, 128]], ALU.is_ge, 0, -1)
+    select(R("tExc"), R("OB"), [[-1, 128]], ALU.is_gt, 0, 1)
+    iota(R("AR"), [[1, 192]], 0, 0)
+    iota(R("DXi"), [[-1, 128]], 0, 1)
+    ts(R("All1"), R("DX", 0, 144), P15, eq)
+    ts(R("IW"), R("DX"), -16.0, eq)
+    ms(R("Bf", V, 3080), V + OFF); ms(R("C", V, 3080), V + OFF); ms(R("X", V, 3280), 255.0)
+    act(R("nba"), R("aw"), ID, bias=-0.5, scale=-1.0)
+    act(R("tf"), R("OB"), ID, bias=200.0, scale=-200.0)
+    act(R("I8"), If, CP, scale=-8.0)
+    act(R("Ib"), If, CP)
+    act(R("In"), If, CP, scale=-1.0)
+    act(H0, H1, ID, bias=1.0, scale=-1.0)
+    act(R("OBn"), R("OB"), CP, scale=-65536.0)
+    act(R("AllP"), R("All1"), CP, scale=131072.0)
+    act(R("AllN"), R("All1"), CP, scale=-65536.0)
+    for e in range(2):
+        for h in range(2):
+            c0 = 16 + 16 * (e - h)
+            act(R("LX", 128 * (2 * e + h), 128 * (2 * e + h + 1)), R("IW", c0, c0 + 128), CP, scale=(H0, H1)[e])
+    cp(R("Tin"), IND(R("Min"), R("prm")))
+    tr(R("Mt"), R("Tin"))
+    for e in range(6):
+        cp(R("Mw", e, 192, 6), R("Mt", 32 * e, 32 * e + 32))
+    send("aMw", nxt, land("Mq", "sMq", last), R("Mw"))
+    if first:
+        select(R("Rf"), R("IW", 0, 128), [[-1, 128]], ALU.not_equal, -112, 1, 1.0)
+        select(R("RfT"), R("IW", 32, 160), [[-1, 128]], ALU.not_equal, 112, 1, 1.0)
+    iota(R("AM"), [[0, 12], [1, 16]], 0, 0)
+    iota(R("IK", 0, 1280), [[0, 1280]], 0, 0)
+    ts(R("F0"), R("Mw", 0, 64), float(V), eq)
+
+    def askers(flags, Wb, fill):
+        scan(R("S1", 8, 72), flags, R("zro"), 0.0, add, mx)
+        mm(P(4, 0, 64), R("OB"), R("S1", 8, 72), True, True)
+        mm(P(5, 0, 64), R("tInc"), R("S1", 8, 72), True, False)
+        mm(P(5, 0, 64), R("tExc"), R("S1", 7, 71), False, True)
+        for c in range(12):
+            act(R("junk", 64 * c, 64 * c + 64), P(4, 0, 64), ACT.Sign, bias=col("nba", c), acc=col("acc", c))
+        cp(R("cnt", 0, 64), P(5, 0, 64))
+        fill[0]()
+        ts(R("b16"), R("acc"), -0.5, mul, 32.0, add)
+        mm(P(6, 0, 12), R("I8"), R("acc"), True, False)
+        tt(R("cmpA"), IND(R("cnt"), R("b16")), R("AR"), ALU.is_le)
+        for q in range(16):
+            mm(P(6, 0, 12), sel("All1", q), R("cmpA", q, 192, 16), False, q == 15)
+        fill[1]()
+        ts(R(Wb, 192, 204), P(6, 0, 12), 512.0, add)
+
+    def rots():
+        ts(R("Dmi"), R("DXi"), 15, ALU.bitwise_and)
+        tt(R("Dm"), R("Dmi"), R("tf"), add)
+        for k in range(9):
+            ts(R("PR", 128 * k, 128 * k + 128), R("Dm"), float(k), eq)
+
+    conv = lambda a, b: ts(R("Bf", a, b), R("Bs", a + a // NS * 8, b + a // NS * 8), OFF, add)
+    askers(R("F0"), "Wo", [rots, lambda: conv(0, NS)])
+    cp(R("Wo", 0, 192), IND(R("Bs", 0, SP), R("Wo", 192, 204)))
+    send("aW", nxt, land("W0", "sW", last), R("Wo"))
+    for k in range(1, 8):
+        act(R("SMa", 128 * (k - 1), 128 * k), R("Dm"), ACT.Abs, bias=-(16 - k) / 2.0)
+    for k in range(1, 8):
+        act(R("SM", 128 * (k - 1), 128 * k), R("SMa", 128 * (k - 1), 128 * k), ACT.Abs, bias=-(16 - k) / 2.0)
+    act(R("SM"), R("SM"), ACT.Relu, bias=1.0, scale=-2.0)
+    if first:
+        act(R("Rb"), R("Rf"), CP)
+    act(CJ, PM, ID, bias=1536.0 - 1048576.0, scale=4096.0)
+    act(NPM, PM, CP, scale=-1.0)
+    act(CG, PM, ID, bias=-8192.0 * 1536)
+    act(CT, P15, CP, scale=-1.0)
+    act(CE, col("mk", 1), ID, bias=24.0, scale=12.0)
+    act(R("OBp"), R("OB"), CP, scale=4096.0)
+    act(R("OBm"), R("OB"), CP, scale=-2048.0)
+    act(R("ZCf"), R("AM"), ACT.Abs, bias=NPM)
+    act(CE, col("mk", 2), ID, bias=CE, scale=-12.0)
+    act(R("selK"), R("OBp"), CP, scale=col("mk", 0))
+    act(R("selI"), R("OB"), CP, scale=col("mk", 1))
+    act(R("ZC"), R("ZCf"), ID, bias=-393216.0, scale=8388608.0)
+    act(R("oEf", 0, 12), R("k12", 0, 12), CP)
+    act(R("oEf", 12, 24), R("k12", 0, 12), ID, bias=CE)
+    act(R("AllS"), R("All1"), CP, scale=0.0625)
+    act(R("IK", V, V + 1), col("mk", 0), CP, scale=-1000.0)
+    for k, d in enumerate((D1, D2, D1)):
+        act(R("D36", 12 * k, 12 * k + 12), R("aw"), ID, bias=float(d))
+    for i in range(16):
+        ts(R("BsH", 144 * i, 144 * i + 144), R("All1"), col("mk", i), mul)
+    conv(NS, 2 * NS)
+    turn_lists("Mq", "sMq", 192, lambda: conv(2 * NS, 2 * NS + 512))
+    conv(2 * NS + 512, V)
+    select(R("PR", 128, 1152), R("PR", 128, 1152), [[0, 8], [-1, 128]], ALU.not_equal, 0, 1, -1.0)
+    select(R("OBh"), R("OBn"), [[0, 8], [-1, 16]], ALU.is_ge, 7, 0)
+    iota(R("IK", 1280, V), [[0, V - 1280]], 0, 0)
+    iota(R("IK", V + 1, 3080), [[0, 3079 - V]], 0, 0)
+    iota(R("rst"), [[0, 192]], int(KMAX), 0)
+    select(R("rst"), R("rst"), [[0, 12], [-1, 16]], ALU.is_ge, 0, 0, -3.0e7)
+    kv = 80 if first else 96
+    act(R("C", 16 * kv, V), IND(R("Bf"), R("Mq", kv, 192)), CP)
+    cp(R("C", 0, 768), IND(R("Bf"), R("Mq", 0, 48)))
+    turn_lists("W0", "sW", 208, lambda: cp(R("C", 768, 16 * kv), IND(R("Bf"), R("Mq", 48, kv))))
+    act(R("Xo", 0, 192), IND(R("X", 0, XW), R("Wo", 192, 204)), CP)
+    send("aU", nxt, land("Xu0", "sXu", last), R("Xo"))
+    iota(R("Ev", NS, V), [[0, 2 * NS]], 0, 0)
+    iota(R("one"), [[0, 192]], 1, 0)
+    iota(R("Cv", 0, 192), [[0, 192]], V + int(OFF), 0)
+    send("aB1", nxt, land("Bp1", "sB1", last), R("Bs", SP, 2 * SP))
+    iota(R("LR2", 0, 192), [[0, 192]], V, 0)
+
+    def rows():
+        cp(R("blf", 0, 384), R("blk", 0, 384))
+        ts(R("blt"), R("blk", 384, 576), float(V), eq, 900.0, mul)
+        tt(R("blf", 384, 576), R("blk", 384, 576), R("blt"), add)
+        dma("s", [(R("IK", 0, V, 1, 0, 128, 16), R("blf", 192, 384)), (R("IK", 0, V, 1, 1, 128, 16), R("blf", 384, 576))])
+        if last:
+            dma("s", [(R("Mr", 0, V, 1, 18, 128, 16), R("blf", 0, 192, 1, 0, 112)), (R("Mr", 0, V, 1, 2, 3), R("blf", 0, 192, 1, 112, 128))])
+        else:
+            dma("s", [(R("Mr", 0, V, 1, 2, 128, 16), R("blf", 0, 192))])
+
+    def lost(t):
+        cp(R("m16", 24 * t, 24 * t + 24), R("LR%d" % t, 384, 408))
+        act(IND(R("Mr"), R("m16", 24 * t, 24 * t + 12)), R("LR2", 0, 192), ACT.Silu)
+
+    def won(t):
+        cp(IND(R("Mr"), R("m16", 24 * t + 12, 24 * t + 24)), R("LR%d" % t, 192, 384))
+
+    def cross(out, src, n):
+        for e in range(2):
+            for h in range(2):
+                mm(P(out, e, n, 2), R("LX", 128 * (2 * e + h), 128 * (2 * e + h + 1)), R(src, h, n, 2), h == 0, h == 1)
+
+    for t in range(RO):
+        W, Xu, GV = "W%d" % t, "Xu%d" % t, "GV%d" % t
+        Cw, Xw = R("C", 0, 3080), R("X", 0, 3088)
+        lo, hi = range(8), range(8, 16)
+        vb, rb = (0, 6, 7), (1, 2, 1)
+        xv = lambda ch, j: R("Xv", 1024 * ch + j, 1024 * ch + 1024, 16)
+        mxs = lambda ch, j, n=1: R("MX", 1024 * ch + 64 * j, 1024 * ch + 64 * (j + n))
+        part = lambda n, ch: R(n, 64 * ch, 64 * ch + 64)
+        key = lambda ch: P(vb[ch], 0, 64)
+
+        def far(a0, a1):
+            ts(R("Y16", 16 * a0, 16 * a1), IND(Cw, R(W, a0, a1)), -1536.0 - OFF, add)
+
+        def pick(ch):
+            for j in range(16):
+                mm(key(ch), sel("BsH", j, (j + t) % 16), R("Y16", 1024 * ch + j, 1024 * ch + 1024, 16), j == 0, j == 15)
+
+        def cand(ch, before=None):
+            ts(part("v16", ch), key(ch), 1536.0, add)
+            act(R("Xv", 1024 * ch, 1024 * ch + 1024), IND(Xw, part("v16", ch)), CP)
+            ts(part("Vh", ch), part("v16", ch), -1536.0, add)
+            if before:
+                before()
+            for k in range(1, 9):
+                mm(P(rb[ch], 64 * k - 64, 64 * k), R("PR", 128 * k, 128 * k + 128), part("Vh", ch), True, True)
+
+        def sup(ch):
+            ts(R("EQ", 512 * ch, 512 * ch + 512), P(rb[ch], 0, 512), 0.0, eq)
+            for k in range(1, 9):
+                c0 = 512 * ch + 64 * k
+                mm(P(3, 64 * ch, 64 * ch + 64), R("SM", 128 * (k - 1), 128 * k) if k < 8 else R("Ib"), R("EQ", c0 - 64, c0), k == 1, k == 8)
+
+        def own():
+            if first:
+                if t:
+                    act(R("sXu", 0, 192), IND(R("sX%d" % t), R("us")), CP)
+                mm(P(5, 0, 192), R("Rb"), R("sXu", 0, 192), True, True)
+                act(R(Xu, 0, 192), P(5, 0, 192), CP)
+            else:
+                if t:
+                    act(R(Xu, 0, 192), IND(R("Xp%d" % t), R(W, 192, 204)), CP)
+                mm(P(5, 0, 192), R("Ib"), R(Xu, 0, 192), True, True)
+
+        def neg(ch, js):
+            for j in js:
+                mm(key(ch), sel("AllN", j), xv(ch, j), j == 0, False)
+
+        def dif(ch, js, b):
+            for n, j in enumerate(js):
+                mm(P(b, 64 * n, 64 * n + 64), R("Ib"), xv(ch, j), True, False)
+                mm(P(b, 64 * n, 64 * n + 64), R("In"), part(Xu, ch), False, True)
+            act(mxs(ch, js[0], 8), P(b, 0, 512), ACT.Abs, scale=0.5)
+
+        def big(ch, js):
+            for j in js:
+                tt(mxs(ch, j), xv(ch, j), P(5, 64 * ch, 64 * ch + 64), mx)
+
+        def pos(ch, js, start=False):
+            for j in js:
+                mm(key(ch), sel("AllP", j), mxs(ch, j), start and j == js[0], False)
+
+        def tail(ch):
+            mm(key(ch), R("Ib"), part("pen", ch), False, False)
+            mm(key(ch), If, part("s2n", ch), False, False)
+            mm(key(ch), R("PR", 0, 128), part("Vh", ch), False, True)
+            tr(part("Tk", ch), key(ch))
+
+        ts(R("uwf"), R(W, 192, 204), float(NS * t), add)
+        far(0, 64)
+        cross(4, "uwf", 12)
+        if first and t:
+            mm(P(2, 0, 12), R("RfT"), R("uwf"), True, True)
+        act(R("Tw", 36, 48), P(4, 0, 12), CP)
+        pick(0)
+        far(64, 96)
+        if first and t:
+            ts(R("us"), P(2, 0, 12), -float(NS * t), add)
+        cand(0)
+        far(96, 128)
+        pick(1)
+        far(128, 160)
+        neg(0, range(16))
+        cand(1)
+        far(160, 192)
+        pick(2)
+        sup(0)
+        own()
+        cand(2, lambda: sup(1))
+        neg(1, lo)
+        dif(1, hi, 4)
+        big(0, lo)
+        sup(2)
+        mm(key(0), R("OBn"), part(Xu, 0), False, False)
+        mm(key(1), R("OBh"), part(Xu, 1), False, False)
+        pos(0, lo)
+        dif(2, lo, 2)
+        act(R("s2n"), P(3, 0, 192), ID, bias=CJ, scale=-1048576.0)
+        act(R("pen"), P(3, 0, 192), ACT.Relu, bias=67108864.0, scale=-67108864.0)
+        dif(2, hi, 1)
+        big(0, hi); big(1, lo)
+        if t == 0:
+            rows()
+            turn("Bp1", "sB1")
+            cp(R("oE"), R("oEf"))
+            ts(R("F12"), R("Mq", 64, 192), float(V), eq)
+        else:
+            if t == 1:
+                turn("Bp2", "sB2")
+            lost(t - 1)
+        pos(1, hi); pos(0, hi); pos(2, lo, True); tail(0); pos(1, lo); tail(1); pos(2, hi); tail(2)
+        scan(R("Sk"), R("rst"), R("Tk"), KMAX, mx, mn)
+        cp(R("ki"), R("Sk", 15, 192, 16))
+        ts(R("vs", 0, 12), R("ki"), 4095, ALU.bitwise_and)
+        ts(R("s16"), R("ki"), 12, ALU.arith_shift_right, -16, ALU.bitwise_and)
+        ts(R("vs", 12, 24), R("ki"), 16, ALU.arith_shift_right)
+        ts(R("v1k"), R("vs", 0, 12), 8192.0, mul, CG, add)
+        cp(R("Tw", 12, 36), R("vs"))
+        tt(R("Tw", 0, 12), R("v1k"), R("s16"), add)
+        cross(2, "Tw", 24)
+        cp(R("E"), IND(R("Tw"), R("oE")))
+        cp(R("QW"), P(2, 0, 24))
+        tr(R(GV, 192, 576), R("E"))
+        cp(R("vw16"), R("QW", 12, 24))
+        act(R("thr"), R("QW", 0, 12), ID, bias=CT)
+        act(R("nhi"), R("QW", 12, 24), ID, bias=8192.0 * 1536 - 4000.0, scale=-8192.0)
+        act(R(GV, 0, 192), R(GV, 192, 384), ID, bias=16.0)
+        act(R("IKg"), IND(R("IK", 0, 3080), R("vw16")), CP)
+        Z = P(3, 0, 192)
+        mm(Z, R("Ib"), R("ZC"), True, False)
+        tt(R("eqd"), IND(R("QW"), R("oE", 0, 12)), R(GV, 192, 384), ALU.is_lt)
+        tt(R("rej"), IND(R("IK", 0, 3080), R("vw16")), R(GV, 384, 576), ALU.is_le)
+        mm(Z, R("OBp"), R("eqd"), False, False)
+        mm(Z, R("selK"), R("rej"), False, False)
+        mm(Z, R("selI"), R("IKg"), False, False)
+        for c in range(12):
+            c0 = 192 * c
+            ts(R("C1", c0, c0 + 176), R(GV, 16 * c + 16, 16 * c + 192), col("thr", c), ALU.is_gt)
+            act(R("C2", c0, c0 + 192), R(GV, 192, 384), ACT.Sign, bias=col("nhi", c))
+            if c < 11:
+                mm(P(3, 16 * c + 16, 192), R("OBp"), R("C1", c0, c0 + 176 - 16 * c), False, False)
+            if c:
+                mm(P(3, 0, 16 * c), R("OBp"), R("C1", c0 + 176 - 16 * c, c0 + 176), False, False)
+            mm(Z, R("OBm"), R("C2", c0, c0 + 192), False, c == 11)
+        if t < RO - 1:
+            act(R("Xv3"), IND(Xw, R("vw16")), CP, scale=3.0)
+            mm(P(7, 0, 192), R("Ib"), R("Xv3"), True, False)
+            mm(P(7, 0, 192), R("Ib"), R(Xu, 0, 192), False, True)
+            act(R("Cv", 192, 384), IND(R("Bf"), R("vw16")), CP)
+            act(R("xr"), P(7, 0, 192), ID, bias=191.625, scale=0.25)
+            act(R("xn"), R("xr"), ID, bias=-192.0)
+        scan(R("SZ"), R("rst"), Z, KMAX, mx, mn)
+        Zw = R("SZ", 15, 192, 16)
+        tt(R(GV, 576, 588), Zw, R("D36", 0, 12), mn)
+        ts(R("L"), Zw, 4096.0, ALU.is_ge, 8192.0, mul)
+        if t < RO - 1:
+            cp(R("o16", 0, 12), R(GV, 576, 588))
+            cp(IND(R("Ev"), R("o16", 0, 12)), R("one"))
+            s0 = NS * (t + 1)
+            mm(P(2, 0, 64), R("Ib"), R("F12", 64 * t, 64 * t + 64), True, False)
+            for q in range(16):
+                mm(P(2, 0, 64), sel("AllS", q), R("Ev", s0 + q, s0 + NS, 16), False, q == 15)
+        tt(R("TT", 0, 12), R("uwf"), R("L"), add)
+        tt(R("TT", 12, 24), R("QW", 12, 24), R("L"), add)
+        tt(R(GV, 588, 612), R("TT"), R("D36", 12, 36), mn)
+        send("aL%d" % t, prv, R("LR%d" % t, 192, 408), R(GV, 384, 600))
+        cp(R("o16", 12, 36), R(GV, 588, 612))
+        keys = lambda: cp(IND(R("IK"), R("o16", 24, 36)), R(GV, 384, 576))
+        if t < RO - 1:
+            def feats():
+                cp(IND(R("X"), R("o16", 24, 36)), R("xn"))
+                send("aX%d" % (t + 1), nxt, land("Xp%d" % (t + 1), "sX%d" % (t + 1), last), R("X", s0, s0 + XW))
+                if t == 0:
+                    send("aB2", nxt, land("Bp2", "sB2", last), R("Bs", 2 * SP, 3 * SP))
+                else:
+                    won(t - 1)
+
+            def tables():
+                act(IND(R("C"), R("o16", 0, 24)), R("Cv"), ACT.Silu)
+                keys()
+            Wn = "W%d" % (t + 1)
+            askers(P(2, 0, 64), Wn, [feats, tables])
+            cp(R(Wn, 0, 192), IND(R("Bp%d" % (t + 1)), R(Wn, 192, 204)))
+        else:
+            keys()
+            dma("s", [(T.yk[:, :], R("IK", 0, V, 1, 0, 128, 16))])
+            won(t - 1)
+            cp(R("m16", 48, 72), R("LR2", 384, 408))
+            cp(IND(R("Mr"), R("m16", 48, 72)), R("LR2", 0, 384))
+            if last:
+                dma("a", [(T.ym[0:7, :], R("Mr", 0, V, 1, 18, 128, 16)), (T.ym[7:8, :], R("Mr", 0, V, 1, 2, 3))])
+            else:
+                dma("a", [(T.ym[:, :], R("Mr", 0, V, 1, 2, 128, 16))])
+    for s in sorted(totals):
+        wait("s", s, totals[s], {})

@@ -1,4 +1,3 @@
-from concourse.bass import DstId, RemoteDMATransfer
 from concourse.mybir import AluOpType as ALU, ActivationFunctionType as ACT
 
 V, NS, RO = 3072, 1024, 3
@@ -11,11 +10,11 @@ KMAX = float(240 * 65536 + V)
 F, H, B, I, U = "float32", "float16", "bfloat16", "int32", "uint16"
 
 _S = {
-    "Min": (192, I), "Tin": (192, F), "Mt": (192, F), "Mw": (192, U), "Mq": (192, U), "sMq": (192, U),
+    "Min": (192, I), "Tin": (192, F), "Mt": (192, F), "Mw": (192, U), "Mq": (192, U), "Mi2": (192, I), "Mw2": (192, U),
     "Bs": (3 * SP, I), "Bf": (3080, F), "C": (TW, F), "Bp1": (SP, I), "Bp2": (SP, I), "sB1": (SP, I), "sB2": (SP, I),
-    "X": (3280, B), "Xp1": (XW, B), "Xp2": (XW, B), "sX1": (XW, B), "sX2": (XW, B),
+    "X": (3280, B), "Xp1": (XW, B), "Xp2": (XW, B),
     "IK": (3280, F), "Mr": (TW, F), "Ev": (3280, B), "blk": (576, I), "blf": (576, F), "blt": (192, F),
-    "Wo": (208, U), "Xo": (208, B), "W0": (208, U), "Xu0": (208, B), "sW": (208, U), "sXu": (208, B), "rf": (208, F),
+    "Wo": (208, U), "Xo": (208, B), "W0": (208, U), "Xu0": (208, B), "sW": (208, U), "rf": (208, F),
     "W1": (208, U), "Xu1": (208, B), "W2": (208, U), "Xu2": (208, B),
     "F0": (64, B), "F12": (128, B), "S1": (80, B), "cnt": (72, F), "junk": (768, B), "cmpA": (192, B),
     "Y16": (3072, H), "v16": (192, U), "Vh": (192, H), "Xv": (3072, B), "MX": (3072, B), "EQ": (1536, B),
@@ -28,12 +27,12 @@ _S = {
     "OB": (128, B), "OBp": (128, B), "OBm": (128, B), "OBn": (128, B), "OBh": (128, B), "tf": (128, F), "Dmi": (128, I), "Dm": (128, B),
     "tInc": (128, B), "tExc": (128, B), "Ib": (128, B), "In": (128, B), "IW": (160, F), "I8": (128, F), "PR": (1152, H),
     "SM": (896, B), "SMa": (896, B), "LX": (512, F), "selK": (128, B), "selI": (128, F), "rst": (192, F), "ZCf": (192, F), "ZC": (192, B),
-    "Rf": (128, F), "RfT": (128, F), "Rb": (128, B), "one": (192, B), "zro": (64, B),
+    "Rf": (128, F), "RfT": (128, F), "Rb": (128, B), "Rn": (128, B), "RO": (128, B), "RH": (128, B), "one": (192, B), "zro": (64, B),
 }
 _SMALL = {F: (("acc", 12), ("uwf", 12), ("v1k", 12), ("Tw", 48), ("QW", 24), ("nhi", 12), ("thr", 12), ("L", 12), ("TT", 24), ("pc", 16),
               ("k12", 16), ("aw", 12), ("nba", 12), ("D36", 36), ("mk", 16), ("pm1", 12), ("oEf", 24)),
           I: (("ki", 12), ("vs", 24), ("s16", 12), ("pI", 1), ("pT", 3)),
-          U: (("b16", 12), ("vw16", 12), ("o16", 36), ("m16", 72), ("prm", 12), ("us", 12), ("oE", 24))}
+          U: (("b16", 12), ("vw16", 12), ("o16", 36), ("m16", 24), ("prm", 12), ("us", 12), ("oE", 24))}
 _AL = {}
 for _d, _l in _SMALL.items():
     _c = 0
@@ -46,7 +45,7 @@ for _k in range(8):
     SCRATCH["P%d" % _k] = ("psum", [128, 512], F)
 
 _DS = ["d%d" % k for k in range(24)]
-_MSG = ["aMw", "aW", "aU", "aB1", "aB2", "aX1", "aX2", "aL0", "aL1", "aL2"]
+_MSG = ["aMw", "aW", "aU", "aB1", "aB2", "aX1", "aX2", "aL0", "aL1", "aL2", "aV"]
 SEMAPHORES = ["qv", "qa", "qp", "qg"] + _DS + _MSG + ["l" + m for m in _MSG]
 
 
@@ -103,9 +102,9 @@ def rank_program(g, core, T, topo):
             for r in regs:
                 psum = r[0] not in _S
                 for (r2, w2, q2, tok, clock) in hist.get(r[0], ()):
-                    if psum and q == "p" and q2 == "p":
+                    if psum and q2 == q and (q == "p" or not (w or w2)):
                         continue
-                    if (w or w2 or (psum and q != q2)) and _meet(r, r2) and need.get(tok[0], (0, None))[0] < tok[1]:
+                    if (w or w2 or psum) and _meet(r, r2) and need.get(tok[0], (0, None))[0] < tok[1]:
                         need[tok[0]] = (tok[1], clock)
         for s, (val_, clock) in sorted(need.items(), key=lambda e: -len(e[1][1])):
             wait(q, s, val_, clock)
@@ -194,26 +193,11 @@ def rank_program(g, core, T, topo):
         g.remote_dma(ap(there), ap(here), T.sem[msg], T.sem["l" + msg], pid, rid, sum(1 << e for e in es))
         note("g", [here], [], ("l" + msg, len(es)))
 
-    def land(final, stage, at_first):
-        return R(stage) if at_first else R(final)
-
-    def turn(final, stage):
-        if first:
-            dma("s", [(R(final, p0=16, p1=128), R(stage, p0=0, p1=112)), (R(final, p0=0, p1=16), R(stage, p0=112, p1=128))])
-
-    def turn_lists(final, stage, n, between=lambda: None):
-        if first:
-            cp(R("rf", 0, n), R(stage, 0, n))
-            mm(P(7, 0, n), R("Rf"), R("rf", 0, n), True, True)
-        between()
-        if first:
-            cp(R(final, 0, n), P(7, 0, n))
-
-    for m, f, s in (("aMw", "Mq", "sMq"), ("aW", "W0", "sW"), ("aU", "Xu0", "sXu"), ("aB1", "Bp1", "sB1"), ("aB2", "Bp2", "sB2"),
-                    ("aX1", "Xp1", "sX1"), ("aX2", "Xp2", "sX2")):
-        note("x", [], [land(f, s, first)], (m, len(engs(prv, core))))
+    for m, f in (("aMw", "Mq"), ("aW", "sW" if first else "W0"), ("aU", "Xu0"), ("aB1", "Bp1"), ("aB2", "Bp2"), ("aX1", "Xp1"), ("aX2", "Xp2")):
+        note("x", [], [R(f)], (m, len(engs(prv, core))))
     for t in range(RO):
-        note("x", [], [R("LR%d" % t, 192, 408)], ("aL%d" % t, len(engs(nxt, core))))
+        note("x", [], [R("LR%d" % t, 384 if t == RO - 1 else 192, 408)], ("aL%d" % t, len(engs(nxt, core))))
+    note("x", [], [R("LR2", 192, 384)], ("aV", len(engs(nxt, core))))
 
     eq, add, mul, mx, mn = ALU.is_equal, ALU.add, ALU.mult, ALU.max, ALU.min
     ID, CP = ACT.Identity, ACT.Copy
@@ -222,14 +206,20 @@ def rank_program(g, core, T, topo):
     sel = lambda n, j, i=0: R(n, 144 * i + 15 - j, 144 * i + 143 - j)
     PM, PG, H1, P15, H0, CJ, NPM, CG, CT, CE = (col("pc", k) for k in range(10))
     If = R("IW", 16, 144)
+    XI, XN, XO, XH = (R(n) for n in (("Rb", "Rn", "RO", "RH") if first else ("Ib", "In", "OBn", "OBh")))
 
     dma("s", [(R("Min", 96 * h, 96 * h + 96), T.mp[h::2, :]) for h in range(2)])
+    if last:
+        dma("s", [(R("Mi2", 96, 192), T.mp[0::2, :]), (R("Mi2", 0, 96, 1, 32, 128), T.mp[1:7:2, :]), (R("Mi2", 0, 96, 1, 0, 32), T.mp[7:8, :])])
     dma("s", [(R("Bs", 0, NS), T.nb[:, 0:NS])])
     dma("s", [(R("Bs", SP, SP + NS), T.nb[:, NS:2 * NS])])
     dma("s", [(R("Bs", 2 * SP, 2 * SP + 512), T.nb[:, 2 * NS:2 * NS + 512])])
     dma("s", [(R("Bs", 2 * SP + 512, 2 * SP + NS), T.nb[:, 2 * NS + 512:3 * NS])])
     dma("s", [(R("X", 0, V), T.x[:, :])])
     dma("s", [(R("blk", 0, 192), T.mp[:, :]), (R("blk", 192, 384), T.ky[:, :]), (R("blk", 384, 576), T.iv[:, :])])
+    if last:
+        for k in (1, 2):
+            dma("s", [(R("sB%d" % k, 0, NS, 1, 16, 128), T.nb[0:112, k * NS:k * NS + NS]), (R("sB%d" % k, 0, NS, 1, 0, 16), T.nb[112:128, k * NS:k * NS + NS])])
 
     iota(R("pI"), [[0, 1]], 0, 1)
     iota(R("pm1"), [[16, 6], [96, 2]], 0, 0)
@@ -271,16 +261,20 @@ def rank_program(g, core, T, topo):
         for h in range(2):
             c0 = 16 + 16 * (e - h)
             act(R("LX", 128 * (2 * e + h), 128 * (2 * e + h + 1)), R("IW", c0, c0 + 128), CP, scale=(H0, H1)[e])
-    cp(R("Tin"), IND(R("Min"), R("prm")))
-    tr(R("Mt"), R("Tin"))
-    for e in range(6):
-        cp(R("Mw", e, 192, 6), R("Mt", 32 * e, 32 * e + 32))
-    send("aMw", nxt, land("Mq", "sMq", last), R("Mw"))
+
+    def wrap(out, src):
+        cp(R("Tin"), IND(R(src), R("prm")))
+        tr(R("Mt"), R("Tin"))
+        for e in range(6):
+            cp(R(out, e, 192, 6), R("Mt", 32 * e, 32 * e + 32))
+
+    wrap("Mw", "Min")
+    if not last:
+        send("aMw", nxt, R("Mq"), R("Mw"))
     if first:
         select(R("Rf"), R("IW", 0, 128), [[-1, 128]], ALU.not_equal, -112, 1, 1.0)
         select(R("RfT"), R("IW", 32, 160), [[-1, 128]], ALU.not_equal, 112, 1, 1.0)
     iota(R("AM"), [[0, 12], [1, 16]], 0, 0)
-    iota(R("IK", 0, 1280), [[0, 1280]], 0, 0)
     ts(R("F0"), R("Mw", 0, 64), float(V), eq)
 
     def askers(flags, Wb, fill):
@@ -290,8 +284,8 @@ def rank_program(g, core, T, topo):
         mm(P(5, 0, 64), R("tExc"), R("S1", 7, 71), False, True)
         for c in range(12):
             act(R("junk", 64 * c, 64 * c + 64), P(4, 0, 64), ACT.Sign, bias=col("nba", c), acc=col("acc", c))
-        cp(R("cnt", 0, 64), P(5, 0, 64))
         fill[0]()
+        cp(R("cnt", 0, 64), P(5, 0, 64))
         ts(R("b16"), R("acc"), -0.5, mul, 32.0, add)
         mm(P(6, 0, 12), R("I8"), R("acc"), True, False)
         tt(R("cmpA"), IND(R("cnt"), R("b16")), R("AR"), ALU.is_le)
@@ -301,15 +295,18 @@ def rank_program(g, core, T, topo):
         ts(R(Wb, 192, 204), P(6, 0, 12), 512.0, add)
 
     def rots():
+        if last:
+            wrap("Mw2", "Mi2")
+            send("aMw", nxt, R("Mq"), R("Mw2"))
         ts(R("Dmi"), R("DXi"), 15, ALU.bitwise_and)
         tt(R("Dm"), R("Dmi"), R("tf"), add)
         for k in range(9):
             ts(R("PR", 128 * k, 128 * k + 128), R("Dm"), float(k), eq)
 
     conv = lambda a, b: ts(R("Bf", a, b), R("Bs", a + a // NS * 8, b + a // NS * 8), OFF, add)
-    askers(R("F0"), "Wo", [rots, lambda: conv(0, NS)])
+    askers(R("F0"), "Wo", [rots, lambda: (iota(R("IK", 0, 768), [[0, 768]], 0, 0), conv(0, NS))])
     cp(R("Wo", 0, 192), IND(R("Bs", 0, SP), R("Wo", 192, 204)))
-    send("aW", nxt, land("W0", "sW", last), R("Wo"))
+    send("aW", nxt, R("sW" if last else "W0"), R("Wo"))
     for k in range(1, 8):
         act(R("SMa", 128 * (k - 1), 128 * k), R("Dm"), ACT.Abs, bias=-(16 - k) / 2.0)
     for k in range(1, 8):
@@ -317,63 +314,72 @@ def rank_program(g, core, T, topo):
     act(R("SM"), R("SM"), ACT.Relu, bias=1.0, scale=-2.0)
     if first:
         act(R("Rb"), R("Rf"), CP)
+        act(R("Rn"), R("Rf"), CP, scale=-1.0)
+        mm(P(7, 0, 128), R("RfT"), R("tf"), True, True)
+        act(R("RO"), P(7, 0, 128), ACT.Sign)
+        act(R("RO"), R("RO"), ID, bias=-65536.0, scale=65536.0)
     act(CJ, PM, ID, bias=1536.0 - 1048576.0, scale=4096.0)
     act(NPM, PM, CP, scale=-1.0)
     act(CG, PM, ID, bias=-8192.0 * 1536)
     act(CT, P15, CP, scale=-1.0)
     act(CE, col("mk", 1), ID, bias=24.0, scale=12.0)
-    act(R("OBp"), R("OB"), CP, scale=4096.0)
-    act(R("OBm"), R("OB"), CP, scale=-2048.0)
-    act(R("ZCf"), R("AM"), ACT.Abs, bias=NPM)
-    act(CE, col("mk", 2), ID, bias=CE, scale=-12.0)
-    act(R("selK"), R("OBp"), CP, scale=col("mk", 0))
-    act(R("selI"), R("OB"), CP, scale=col("mk", 1))
-    act(R("ZC"), R("ZCf"), ID, bias=-393216.0, scale=8388608.0)
     act(R("oEf", 0, 12), R("k12", 0, 12), CP)
-    act(R("oEf", 12, 24), R("k12", 0, 12), ID, bias=CE)
-    act(R("AllS"), R("All1"), CP, scale=0.0625)
+    act(CE, col("mk", 2), ID, bias=CE, scale=-12.0)
     act(R("IK", V, V + 1), col("mk", 0), CP, scale=-1000.0)
-    for k, d in enumerate((D1, D2, D1)):
-        act(R("D36", 12 * k, 12 * k + 12), R("aw"), ID, bias=float(d))
+    act(R("oEf", 12, 24), R("k12", 0, 12), ID, bias=CE)
+
+    def later():
+        act(R("OBp"), R("OB"), CP, scale=4096.0)
+        act(R("OBm"), R("OB"), CP, scale=-2048.0)
+        act(R("ZCf"), R("AM"), ACT.Abs, bias=NPM)
+        act(R("selK"), R("OBp"), CP, scale=col("mk", 0))
+        act(R("selI"), R("OB"), CP, scale=col("mk", 1))
+        act(R("ZC"), R("ZCf"), ID, bias=-393216.0, scale=8388608.0)
+        act(R("AllS"), R("All1"), CP, scale=0.0625)
+        for k, d in enumerate((D1, D2, D1)):
+            act(R("D36", 12 * k, 12 * k + 12), R("aw"), ID, bias=float(d))
+
     for i in range(16):
         ts(R("BsH", 144 * i, 144 * i + 144), R("All1"), col("mk", i), mul)
     conv(NS, 2 * NS)
-    turn_lists("Mq", "sMq", 192, lambda: conv(2 * NS, 2 * NS + 512))
+    conv(2 * NS, 2 * NS + 512)
     conv(2 * NS + 512, V)
     select(R("PR", 128, 1152), R("PR", 128, 1152), [[0, 8], [-1, 128]], ALU.not_equal, 0, 1, -1.0)
-    select(R("OBh"), R("OBn"), [[0, 8], [-1, 16]], ALU.is_ge, 7, 0)
-    iota(R("IK", 1280, V), [[0, V - 1280]], 0, 0)
+    select(XH, XO, [[0, 8], [-1, 16]], ALU.is_ge, 7, 0)
+    iota(R("IK", 768, V), [[0, V - 768]], 0, 0)
+    kv = 84 if first else 96
+    act(R("C", 16 * kv, V), IND(R("Bf"), R("Mq", kv, 192)), CP)
+    cp(R("C", 0, 768), IND(R("Bf"), R("Mq", 0, 48)))
+    if first:
+        cp(R("rf"), R("sW"))
+        mm(P(7, 0, 208), R("Rf"), R("rf"), True, True)
+    cp(R("C", 768, 16 * kv), IND(R("Bf"), R("Mq", 48, kv)))
+    if first:
+        cp(R("W0"), P(7, 0, 208))
+    act(R("Xo", 0, 192), IND(R("X", 0, XW), R("Wo", 192, 204)), CP)
+    send("aU", nxt, R("Xu0"), R("Xo"))
+    later()
     iota(R("IK", V + 1, 3080), [[0, 3079 - V]], 0, 0)
     iota(R("rst"), [[0, 192]], int(KMAX), 0)
     select(R("rst"), R("rst"), [[0, 12], [-1, 16]], ALU.is_ge, 0, 0, -3.0e7)
-    kv = 80 if first else 96
-    act(R("C", 16 * kv, V), IND(R("Bf"), R("Mq", kv, 192)), CP)
-    cp(R("C", 0, 768), IND(R("Bf"), R("Mq", 0, 48)))
-    turn_lists("W0", "sW", 208, lambda: cp(R("C", 768, 16 * kv), IND(R("Bf"), R("Mq", 48, kv))))
-    act(R("Xo", 0, 192), IND(R("X", 0, XW), R("Wo", 192, 204)), CP)
-    send("aU", nxt, land("Xu0", "sXu", last), R("Xo"))
+    if last:
+        iota(R("sB1", NS, SP), [[0, 8]], V, 0); iota(R("sB2", NS, SP), [[0, 8]], V, 0)
+    send("aB1", nxt, R("Bp1"), R("sB1") if last else R("Bs", SP, 2 * SP))
     iota(R("Ev", NS, V), [[0, 2 * NS]], 0, 0)
     iota(R("one"), [[0, 192]], 1, 0)
     iota(R("Cv", 0, 192), [[0, 192]], V + int(OFF), 0)
-    send("aB1", nxt, land("Bp1", "sB1", last), R("Bs", SP, 2 * SP))
     iota(R("LR2", 0, 192), [[0, 192]], V, 0)
 
     def rows():
         cp(R("blf", 0, 384), R("blk", 0, 384))
         ts(R("blt"), R("blk", 384, 576), float(V), eq, 900.0, mul)
+        cp(R("oE"), R("oEf"))
         tt(R("blf", 384, 576), R("blk", 384, 576), R("blt"), add)
         dma("s", [(R("IK", 0, V, 1, 0, 128, 16), R("blf", 192, 384)), (R("IK", 0, V, 1, 1, 128, 16), R("blf", 384, 576))])
         if last:
             dma("s", [(R("Mr", 0, V, 1, 18, 128, 16), R("blf", 0, 192, 1, 0, 112)), (R("Mr", 0, V, 1, 2, 3), R("blf", 0, 192, 1, 112, 128))])
         else:
             dma("s", [(R("Mr", 0, V, 1, 2, 128, 16), R("blf", 0, 192))])
-
-    def lost(t):
-        cp(R("m16", 24 * t, 24 * t + 24), R("LR%d" % t, 384, 408))
-        act(IND(R("Mr"), R("m16", 24 * t, 24 * t + 12)), R("LR2", 0, 192), ACT.Silu)
-
-    def won(t):
-        cp(IND(R("Mr"), R("m16", 24 * t + 12, 24 * t + 24)), R("LR%d" % t, 192, 384))
 
     def cross(out, src, n):
         for e in range(2):
@@ -400,7 +406,7 @@ def rank_program(g, core, T, topo):
         def cand(ch, before=None):
             ts(part("v16", ch), key(ch), 1536.0, add)
             act(R("Xv", 1024 * ch, 1024 * ch + 1024), IND(Xw, part("v16", ch)), CP)
-            ts(part("Vh", ch), part("v16", ch), -1536.0, add)
+            ts(part("Vh", ch), key(ch), 12582912.0, add, -12582912.0, add)
             if before:
                 before()
             for k in range(1, 9):
@@ -413,15 +419,9 @@ def rank_program(g, core, T, topo):
                 mm(P(3, 64 * ch, 64 * ch + 64), R("SM", 128 * (k - 1), 128 * k) if k < 8 else R("Ib"), R("EQ", c0 - 64, c0), k == 1, k == 8)
 
         def own():
-            if first:
-                if t:
-                    act(R("sXu", 0, 192), IND(R("sX%d" % t), R("us")), CP)
-                mm(P(5, 0, 192), R("Rb"), R("sXu", 0, 192), True, True)
-                act(R(Xu, 0, 192), P(5, 0, 192), CP)
-            else:
-                if t:
-                    act(R(Xu, 0, 192), IND(R("Xp%d" % t), R(W, 192, 204)), CP)
-                mm(P(5, 0, 192), R("Ib"), R(Xu, 0, 192), True, True)
+            if t:
+                act(R(Xu, 0, 192), IND(R("Xp%d" % t), R("us") if first else R(W, 192, 204)), CP)
+            mm(P(5, 0, 192), XI, R(Xu, 0, 192), True, True)
 
         def neg(ch, js):
             for j in js:
@@ -430,7 +430,7 @@ def rank_program(g, core, T, topo):
         def dif(ch, js, b):
             for n, j in enumerate(js):
                 mm(P(b, 64 * n, 64 * n + 64), R("Ib"), xv(ch, j), True, False)
-                mm(P(b, 64 * n, 64 * n + 64), R("In"), part(Xu, ch), False, True)
+                mm(P(b, 64 * n, 64 * n + 64), XN, part(Xu, ch), False, True)
             act(mxs(ch, js[0], 8), P(b, 0, 512), ACT.Abs, scale=0.5)
 
         def big(ch, js):
@@ -447,7 +447,10 @@ def rank_program(g, core, T, topo):
             mm(key(ch), R("PR", 0, 128), part("Vh", ch), False, True)
             tr(part("Tk", ch), key(ch))
 
-        ts(R("uwf"), R(W, 192, 204), float(NS * t), add)
+        if t == 0:
+            cp(R("uwf"), R(W, 192, 204))
+        else:
+            lr = "LR%d" % (t - 1)
         far(0, 64)
         cross(4, "uwf", 12)
         if first and t:
@@ -472,23 +475,22 @@ def rank_program(g, core, T, topo):
         dif(1, hi, 4)
         big(0, lo)
         sup(2)
-        mm(key(0), R("OBn"), part(Xu, 0), False, False)
-        mm(key(1), R("OBh"), part(Xu, 1), False, False)
+        mm(key(0), XO, part(Xu, 0), False, False)
+        mm(key(1), XH, part(Xu, 1), False, False)
         pos(0, lo)
         dif(2, lo, 2)
         act(R("s2n"), P(3, 0, 192), ID, bias=CJ, scale=-1048576.0)
         act(R("pen"), P(3, 0, 192), ACT.Relu, bias=67108864.0, scale=-67108864.0)
         dif(2, hi, 1)
+        if t:
+            cp(R("m16"), R(lr, 384, 408))
         big(0, hi); big(1, lo)
         if t == 0:
             rows()
-            turn("Bp1", "sB1")
-            cp(R("oE"), R("oEf"))
             ts(R("F12"), R("Mq", 64, 192), float(V), eq)
         else:
-            if t == 1:
-                turn("Bp2", "sB2")
-            lost(t - 1)
+            cp(IND(R("Mr"), R("m16", 12, 24)), R(lr, 192, 384))
+            act(IND(R("Mr"), R("m16", 0, 12)), R("LR2", 0, 192), ACT.Silu)
         pos(1, hi); pos(0, hi); pos(2, lo, True); tail(0); pos(1, lo); tail(1); pos(2, hi); tail(2)
         scan(R("Sk"), R("rst"), R("Tk"), KMAX, mx, mn)
         cp(R("ki"), R("Sk", 15, 192, 16))
@@ -501,8 +503,10 @@ def rank_program(g, core, T, topo):
         cross(2, "Tw", 24)
         cp(R("E"), IND(R("Tw"), R("oE")))
         cp(R("QW"), P(2, 0, 24))
+        cp(R("vw16"), P(2, 12, 24))
         tr(R(GV, 192, 576), R("E"))
-        cp(R("vw16"), R("QW", 12, 24))
+        if t == RO - 1:
+            send("aV", prv, R("LR2", 192, 384), R(GV, 384, 576))
         act(R("thr"), R("QW", 0, 12), ID, bias=CT)
         act(R("nhi"), R("QW", 12, 24), ID, bias=8192.0 * 1536 - 4000.0, scale=-8192.0)
         act(R(GV, 0, 192), R(GV, 192, 384), ID, bias=16.0)
@@ -526,7 +530,7 @@ def rank_program(g, core, T, topo):
         if t < RO - 1:
             act(R("Xv3"), IND(Xw, R("vw16")), CP, scale=3.0)
             mm(P(7, 0, 192), R("Ib"), R("Xv3"), True, False)
-            mm(P(7, 0, 192), R("Ib"), R(Xu, 0, 192), False, True)
+            mm(P(7, 0, 192), XI, R(Xu, 0, 192), False, True)
             act(R("Cv", 192, 384), IND(R("Bf"), R("vw16")), CP)
             act(R("xr"), P(7, 0, 192), ID, bias=191.625, scale=0.25)
             act(R("xn"), R("xr"), ID, bias=-192.0)
@@ -536,38 +540,40 @@ def rank_program(g, core, T, topo):
         ts(R("L"), Zw, 4096.0, ALU.is_ge, 8192.0, mul)
         if t < RO - 1:
             cp(R("o16", 0, 12), R(GV, 576, 588))
+            tt(R("TT", 0, 12), R("uwf"), R("L"), add)
             cp(IND(R("Ev"), R("o16", 0, 12)), R("one"))
+            act(IND(R("C"), R("o16", 0, 12)), R("Cv", 0, 192), ACT.Silu)
             s0 = NS * (t + 1)
             mm(P(2, 0, 64), R("Ib"), R("F12", 64 * t, 64 * t + 64), True, False)
             for q in range(16):
                 mm(P(2, 0, 64), sel("AllS", q), R("Ev", s0 + q, s0 + NS, 16), False, q == 15)
-        tt(R("TT", 0, 12), R("uwf"), R("L"), add)
+        else:
+            tt(R("TT", 0, 12), R("uwf"), R("L"), add)
         tt(R("TT", 12, 24), R("QW", 12, 24), R("L"), add)
         tt(R(GV, 588, 612), R("TT"), R("D36", 12, 36), mn)
-        send("aL%d" % t, prv, R("LR%d" % t, 192, 408), R(GV, 384, 600))
+        c0 = 192 if t == RO - 1 else 0
+        send("aL%d" % t, prv, R("LR%d" % t, 192 + c0, 408), R(GV, 384 + c0, 600))
         cp(R("o16", 12, 36), R(GV, 588, 612))
         keys = lambda: cp(IND(R("IK"), R("o16", 24, 36)), R(GV, 384, 576))
         if t < RO - 1:
             def feats():
                 cp(IND(R("X"), R("o16", 24, 36)), R("xn"))
-                send("aX%d" % (t + 1), nxt, land("Xp%d" % (t + 1), "sX%d" % (t + 1), last), R("X", s0, s0 + XW))
+                send("aX%d" % (t + 1), nxt, R("Xp%d" % (t + 1)), R("X", s0, s0 + XW))
                 if t == 0:
-                    send("aB2", nxt, land("Bp2", "sB2", last), R("Bs", 2 * SP, 3 * SP))
-                else:
-                    won(t - 1)
+                    send("aB2", nxt, R("Bp2"), R("sB2") if last else R("Bs", 2 * SP, 3 * SP))
 
             def tables():
-                act(IND(R("C"), R("o16", 0, 24)), R("Cv"), ACT.Silu)
+                act(IND(R("C"), R("o16", 12, 24)), R("Cv", 192, 384), ACT.Silu)
                 keys()
             Wn = "W%d" % (t + 1)
             askers(P(2, 0, 64), Wn, [feats, tables])
+            ts(R("uwf"), P(6, 0, 12), 512.0 + s0, add)
             cp(R(Wn, 0, 192), IND(R("Bp%d" % (t + 1)), R(Wn, 192, 204)))
         else:
             keys()
             dma("s", [(T.yk[:, :], R("IK", 0, V, 1, 0, 128, 16))])
-            won(t - 1)
-            cp(R("m16", 48, 72), R("LR2", 384, 408))
-            cp(IND(R("Mr"), R("m16", 48, 72)), R("LR2", 0, 384))
+            cp(R("m16"), R("LR2", 384, 408))
+            cp(IND(R("Mr"), R("m16")), R("LR2", 0, 384))
             if last:
                 dma("a", [(T.ym[0:7, :], R("Mr", 0, V, 1, 18, 128, 16)), (T.ym[7:8, :], R("Mr", 0, V, 1, 2, 3))])
             else:

from concourse.mybir import AluOpType as ALU, ActivationFunctionType as ACT

V, NS, RO = 3072, 1024, 3
SP = NS + 8
XW = NS + 16
D1, D2 = 3080, 3272
TW = 3472
OFF = 64.0
KMAX = float(240 * 65536 + V)
F, H, B, I, U = "float32", "float16", "bfloat16", "int32", "uint16"

_S = {
    "Min": (192, I), "Tin": (192, F), "Mt": (192, F), "Mw": (192, U), "Mq": (192, U), "Mi2": (192, I), "Mw2": (192, U),
    "Bs": (3 * SP, I), "Bf": (3080, F), "C": (TW, F), "Bp1": (SP, I), "Bp2": (SP, I), "sB1": (SP, I), "sB2": (SP, I),
    "X": (3280, B), "Xp1": (XW, B), "Xp2": (XW, B),
    "IK": (3280, F), "Mr": (TW, F), "Ev": (3280, B), "blk": (576, I), "blf": (576, F), "blt": (192, F),
    "Wo": (208, U), "Xo": (208, B), "W0": (208, U), "Xu0": (208, B), "sW": (208, U), "rf": (208, F),
    "W1": (208, U), "Xu1": (208, B), "W2": (208, U), "Xu2": (208, B),
    "F0": (64, B), "F12": (128, B), "S1": (80, B), "cnt": (72, F), "junk": (768, B), "cmpA": (192, B),
    "Y16": (3072, H), "v16": (192, U), "Vh": (192, H), "Xv": (3072, B), "MX": (3072, B), "EQ": (1536, B),
    "s2n": (192, F), "pen": (192, B), "Tk": (192, F), "Sk": (192, F),
    "E": (384, F), "GV0": (616, F), "GV1": (616, F), "GV2": (616, F),
    "IKg": (192, F), "rej": (192, B), "C1": (2304, B), "C2": (2304, B), "eqd": (192, B), "SZ": (192, F),
    "Xv3": (192, B), "xr": (192, B), "xn": (192, B), "Cv": (384, F), "LR0": (408, F), "LR1": (408, F), "LR2": (408, F),
    "DXi": (128, I), "DX": (160, F), "Gx": (128, F), "AM": (192, F), "AR": (192, F),
    "All1": (144, B), "AllP": (144, B), "AllN": (144, B), "AllS": (144, B), "BsH": (2304, H),
    "OB": (128, B), "OBp": (128, B), "OBm": (128, B), "OBn": (128, B), "OBh": (128, B), "tf": (128, F), "Dmi": (128, I), "Dm": (128, B),
    "tInc": (128, B), "tExc": (128, B), "Ib": (128, B), "In": (128, B), "IW": (160, F), "I8": (128, F), "PR": (1152, H),
    "SM": (896, B), "SMa": (896, B), "LX": (512, F), "selK": (128, B), "selI": (128, F), "rst": (192, F), "ZCf": (192, F), "ZC": (192, B),
    "Rf": (128, F), "RfT": (128, F), "Rb": (128, B), "Rn": (128, B), "RO": (128, B), "RH": (128, B), "one": (192, B), "zro": (64, B),
}
_SMALL = {F: (("acc", 12), ("uwf", 12), ("v1k", 12), ("Tw", 48), ("QW", 24), ("nhi", 12), ("thr", 12), ("L", 12), ("TT", 24), ("pc", 16),
              ("k12", 16), ("aw", 12), ("nba", 12), ("D36", 36), ("mk", 16), ("pm1", 12), ("oEf", 24)),
          I: (("ki", 12), ("vs", 24), ("s16", 12), ("pI", 1), ("pT", 3)),
          U: (("b16", 12), ("vw16", 12), ("o16", 36), ("m16", 24), ("prm", 12), ("us", 12), ("oE", 24))}
_AL = {}
for _d, _l in _SMALL.items():
    _c = 0
    for _n, _w in _l:
        _AL[_n] = ("sm" + _d, _c, _w)
        _c += (_w + 15) // 16 * 16
    _S["sm" + _d] = (_c, _d)
SCRATCH = {k: ("sbuf", [128, w], d) for k, (w, d) in _S.items()}
for _k in range(8):
    SCRATCH["P%d" % _k] = ("psum", [128, 512], F)

_DS = ["d%d" % k for k in range(24)]
_MSG = ["aMw", "aW", "aU", "aB1", "aB2", "aX1", "aX2", "aL0", "aL1", "aL2", "aV"]
SEMAPHORES = ["qv", "qa", "qp", "qg"] + _DS + _MSG + ["l" + m for m in _MSG]


def R(name, c0=0, c1=None, cs=1, p0=0, p1=128, ps=1):
    if name in _AL:
        base, o, w = _AL[name]
        return (base, o + c0, o + (w if c1 is None else c1), cs, p0, p1, ps)
    return (name, c0, _S[name][0] if c1 is None else c1, cs, p0, p1, ps)


def IND(win, off):
    return ("*", win, off)


def _meet(a, b):
    if a[0] not in _S:
        return True
    if a[3] > 1 and a[3] == b[3] and (a[1] - b[1]) % a[3]:
        return False
    return a[1] < b[2] and b[1] < a[2] and a[4] < b[5] and b[4] < a[5]


def rank_program(g, core, T, topo):
    rank = T.rank_of(core)
    if rank is None:
        return
    N = len(T.cores)
    nxt, prv = T.cores[(rank + 1) % N], T.cores[(rank - 1) % N]
    first, last = rank == 0, rank == N - 1
    Q = {"v": g.vector, "a": g.scalar, "p": g.tensor, "g": g, "s": g.sync}
    count = {"v": 0, "a": 0, "p": 0, "g": 0}
    known = {q: {} for q in Q}
    hist = {}
    totals = {}
    nd = [0]

    def ap(r):
        if r[0] == "*":
            return ap(r[1]).indirect(ap(r[2]))
        n, c0, c1, cs, p0, p1, ps = r
        return T[n][p0:p1:ps, c0:c1:cs] if (cs > 1 or ps > 1) else T[n][p0:p1, c0:c1]

    def wait(q, sem, val, clock):
        if known[q].get(sem, 0) < val:
            Q[q].wait_ge(T.sem[sem], val)
            known[q][sem] = val
            for s, x in clock.items():
                if known[q].get(s, 0) < x:
                    known[q][s] = x

    def order(q, reads, writes):
        need = {}
        for regs, w in ((reads, False), (writes, True)):
            for r in regs:
                psum = r[0] not in _S
                for (r2, w2, q2, tok, clock) in hist.get(r[0], ()):
                    if psum and q2 == q and (q == "p" or not (w or w2)):
                        continue
                    if (w or w2 or psum) and _meet(r, r2) and need.get(tok[0], (0, None))[0] < tok[1]:
                        need[tok[0]] = (tok[1], clock)
        for s, (val_, clock) in sorted(need.items(), key=lambda e: -len(e[1][1])):
            wait(q, s, val_, clock)

    def note(q, reads, writes, tok):
        clock = dict(known[q]) if q in known else {}
        totals[tok[0]] = max(totals.get(tok[0], 0), tok[1])
        for regs, w in ((reads, False), (writes, True)):
            for r in regs:
                hist.setdefault(r[0], []).append((r, w, q, tok, clock))

    def op(q, out, ins, fn, more=()):
        reads, writes = [], list(more)
        for r in ins:
            if isinstance(r, tuple):
                reads += [r[1], r[2]] if r[0] == "*" else [r]
        if out[0] == "*":
            writes.append(out[1]); reads.append(out[2])
        else:
            writes.append(out)
        order(q, reads, writes)
        count[q] += 1
        fn().then_inc(T.sem["q" + q], 1)
        note(q, reads, writes, ("q" + q, count[q]))

    def val(x):
        return ap(x) if isinstance(x, tuple) else x

    def cp(out, in_):
        op("v", out, [in_], lambda: g.vector.tensor_copy(ap(out), ap(in_)))

    def tt(out, a, b, o):
        op("v", out, [a, b], lambda: g.vector.tensor_tensor(ap(out), ap(a), ap(b), o))

    def ts(out, a, s1, o0, s2=None, o1=None):
        if o1 is None:
            op("v", out, [a, s1], lambda: g.vector.tensor_scalar(ap(out), ap(a), val(s1), None, o0))
        else:
            op("v", out, [a, s1, s2], lambda: g.vector.tensor_scalar(ap(out), ap(a), val(s1), val(s2), o0, o1))

    def scan(out, d0, d1, init, o0, o1):
        op("v", out, [d0, d1], lambda: g.vector.tensor_tensor_scan(ap(out), ap(d0), ap(d1), init, o0, o1))

    def tr(out, in_):
        op("v", out, [in_], lambda: g.vector.transpose(ap(out), ap(in_)))

    def ms(out, c):
        op("v", out, [], lambda: g.vector.memset(ap(out), c))

    def act(out, in_, f, bias=0.0, scale=1.0, acc=None):
        if out[0] == "*":
            op("a", out, [in_], lambda: g.scalar.activation(ap(out), ap(in_), f))
        elif acc is None:
            op("a", out, [in_, bias, scale], lambda: g.scalar.activation(ap(out), ap(in_), f, bias=val(bias), scale=val(scale)))
        else:
            op("a", out, [in_, bias, scale], lambda: g.scalar.activation(ap(out), ap(in_), f, bias=val(bias), scale=val(scale), accum_out=ap(acc)), [acc])

    def mm(out, lhsT, rhs, start, stop):
        op("p", out, [lhsT, rhs], lambda: g.tensor.matmul(ap(out), ap(lhsT), ap(rhs), start, stop))

    def iota(out, pattern, base, cm):
        if _S[out[0]][1] == I:
            op("g", out, [], lambda: g.iota(ap(out), pattern, base, cm))
        else:
            op("g", out, [], lambda: g.iota(ap(out), pattern, base, cm, allow_small_or_imprecise_dtypes=True))

    def select(out, in_, pattern, cmp, base, cm, fill=0.0):
        op("g", out, [in_], lambda: g.affine_select(ap(out), ap(in_), pattern, cmp, fill, base, cm))

    def dma(q, pairs):
        sem = _DS[nd[0]]; nd[0] += 1
        reads = [s for d, s in pairs if isinstance(s, tuple)]
        writes = [d for d, s in pairs if isinstance(d, tuple)]
        order(q, reads, writes)
        for d, s in pairs:
            Q[q].dma_start(val(d), val(s)).then_inc(T.sem[sem], 16)
        note(q, reads, writes, (sem, 16 * len(pairs)))

    def engs(src, dst):
        return topo.engines(src, dst)[:8]

    def send(msg, dst, there, here):
        order("g", [here], [])
        rid, pid = topo.addr(dst)[:2]
        es = engs(core, dst)
        g.remote_dma(ap(there), ap(here), T.sem[msg], T.sem["l" + msg], pid, rid, sum(1 << e for e in es))
        note("g", [here], [], ("l" + msg, len(es)))

    for m, f in (("aMw", "Mq"), ("aW", "sW" if first else "W0"), ("aU", "Xu0"), ("aB1", "Bp1"), ("aB2", "Bp2"), ("aX1", "Xp1"), ("aX2", "Xp2")):
        note("x", [], [R(f)], (m, len(engs(prv, core))))
    for t in range(RO):
        note("x", [], [R("LR%d" % t, 384 if t == RO - 1 else 192, 408)], ("aL%d" % t, len(engs(nxt, core))))
    note("x", [], [R("LR2", 192, 384)], ("aV", len(engs(nxt, core))))

    eq, add, mul, mx, mn = ALU.is_equal, ALU.add, ALU.mult, ALU.max, ALU.min
    ID, CP = ACT.Identity, ACT.Copy
    col = lambda n, c: R(n, c, c + 1)
    P = lambda k, c0, c1, cs=1: ("P%d" % k, c0, c1, cs, 0, 128, 1)
    sel = lambda n, j, i=0: R(n, 144 * i + 15 - j, 144 * i + 143 - j)
    PM, PG, H1, P15, H0, CJ, NPM, CG, CT, CE = (col("pc", k) for k in range(10))
    If = R("IW", 16, 144)
    XI, XN, XO, XH = (R(n) for n in (("Rb", "Rn", "RO", "RH") if first else ("Ib", "In", "OBn", "OBh")))

    dma("s", [(R("Min", 96 * h, 96 * h + 96), T.mp[h::2, :]) for h in range(2)])
    if last:
        dma("s", [(R("Mi2", 96, 192), T.mp[0::2, :]), (R("Mi2", 0, 96, 1, 32, 128), T.mp[1:7:2, :]), (R("Mi2", 0, 96, 1, 0, 32), T.mp[7:8, :])])
    dma("s", [(R("Bs", 0, NS), T.nb[:, 0:NS])])
    dma("s", [(R("Bs", SP, SP + NS), T.nb[:, NS:2 * NS])])
    dma("s", [(R("Bs", 2 * SP, 2 * SP + 512), T.nb[:, 2 * NS:2 * NS + 512])])
    dma("s", [(R("Bs", 2 * SP + 512, 2 * SP + NS), T.nb[:, 2 * NS + 512:3 * NS])])
    dma("s", [(R("X", 0, V), T.x[:, :])])
    dma("s", [(R("blk", 0, 192), T.mp[:, :]), (R("blk", 192, 384), T.ky[:, :]), (R("blk", 384, 576), T.iv[:, :])])
    if last:
        for k in (1, 2):
            dma("s", [(R("sB%d" % k, 0, NS, 1, 16, 128), T.nb[0:112, k * NS:k * NS + NS]), (R("sB%d" % k, 0, NS, 1, 0, 16), T.nb[112:128, k * NS:k * NS + NS])])

    iota(R("pI"), [[0, 1]], 0, 1)
    iota(R("pm1"), [[16, 6], [96, 2]], 0, 0)
    iota(R("Gx"), [[1, 8], [0, 16]], 0, 0)
    iota(R("k12"), [[1, 16]], 0, 0)
    iota(R("DX"), [[-1, 160]], 0, 1)
    ms(R("zro"), 0.0)
    ms(R("S1", 0, 8), 0.0)
    ms(R("cnt", 64, 72), 30000.0)
    ts(col("pT", 0), R("pI"), 15, ALU.bitwise_and)
    ts(col("pT", 1), R("pI"), 4, ALU.arith_shift_right)
    ts(col("pT", 2), R("pI"), 4, ALU.arith_shift_right, 1, ALU.bitwise_and)
    for k in range(3):
        ms(R("Bs", k * SP + NS, k * SP + SP), V)
    cp(R("pc", 0, 3), R("pT"))
    ms(R("Wo", 204, 208), 0); ms(R("Xo", 192, 208), 0.0)
    ts(R("prm"), R("pm1"), PM, add)
    ts(R("OB"), R("Gx"), PG, eq)
    ts(P15, PM, -15.0, add)
    ts(R("aw"), R("k12", 0, 12), 16.0, mul, PM, add)
    ts(R("mk"), R("k12"), PM, eq)
    select(R("tInc"), R("OB"), [[1, 128]], ALU.is_ge, 0, -1)
    select(R("tExc"), R("OB"), [[-1, 128]], ALU.is_gt, 0, 1)
    iota(R("AR"), [[1, 192]], 0, 0)
    iota(R("DXi"), [[-1, 128]], 0, 1)
    ts(R("All1"), R("DX", 0, 144), P15, eq)
    ts(R("IW"), R("DX"), -16.0, eq)
    ms(R("Bf", V, 3080), V + OFF); ms(R("C", V, 3080), V + OFF); ms(R("X", V, 3280), 255.0)
    act(R("nba"), R("aw"), ID, bias=-0.5, scale=-1.0)
    act(R("tf"), R("OB"), ID, bias=200.0, scale=-200.0)
    act(R("I8"), If, CP, scale=-8.0)
    act(R("Ib"), If, CP)
    act(R("In"), If, CP, scale=-1.0)
    act(H0, H1, ID, bias=1.0, scale=-1.0)
    act(R("OBn"), R("OB"), CP, scale=-65536.0)
    act(R("AllP"), R("All1"), CP, scale=131072.0)
    act(R("AllN"), R("All1"), CP, scale=-65536.0)
    for e in range(2):
        for h in range(2):
            c0 = 16 + 16 * (e - h)
            act(R("LX", 128 * (2 * e + h), 128 * (2 * e + h + 1)), R("IW", c0, c0 + 128), CP, scale=(H0, H1)[e])

    def wrap(out, src):
        cp(R("Tin"), IND(R(src), R("prm")))
        tr(R("Mt"), R("Tin"))
        for e in range(6):
            cp(R(out, e, 192, 6), R("Mt", 32 * e, 32 * e + 32))

    wrap("Mw", "Min")
    if not last:
        send("aMw", nxt, R("Mq"), R("Mw"))
    if first:
        select(R("Rf"), R("IW", 0, 128), [[-1, 128]], ALU.not_equal, -112, 1, 1.0)
        select(R("RfT"), R("IW", 32, 160), [[-1, 128]], ALU.not_equal, 112, 1, 1.0)
    iota(R("AM"), [[0, 12], [1, 16]], 0, 0)
    ts(R("F0"), R("Mw", 0, 64), float(V), eq)

    def askers(flags, Wb, fill):
        scan(R("S1", 8, 72), flags, R("zro"), 0.0, add, mx)
        mm(P(4, 0, 64), R("OB"), R("S1", 8, 72), True, True)
        mm(P(5, 0, 64), R("tInc"), R("S1", 8, 72), True, False)
        mm(P(5, 0, 64), R("tExc"), R("S1", 7, 71), False, True)
        for c in range(12):
            act(R("junk", 64 * c, 64 * c + 64), P(4, 0, 64), ACT.Sign, bias=col("nba", c), acc=col("acc", c))
        fill[0]()
        cp(R("cnt", 0, 64), P(5, 0, 64))
        ts(R("b16"), R("acc"), -0.5, mul, 32.0, add)
        mm(P(6, 0, 12), R("I8"), R("acc"), True, False)
        tt(R("cmpA"), IND(R("cnt"), R("b16")), R("AR"), ALU.is_le)
        for q in range(16):
            mm(P(6, 0, 12), sel("All1", q), R("cmpA", q, 192, 16), False, q == 15)
        fill[1]()
        ts(R(Wb, 192, 204), P(6, 0, 12), 512.0, add)

    def rots():
        if last:
            wrap("Mw2", "Mi2")
            send("aMw", nxt, R("Mq"), R("Mw2"))
        ts(R("Dmi"), R("DXi"), 15, ALU.bitwise_and)
        tt(R("Dm"), R("Dmi"), R("tf"), add)
        for k in range(9):
            ts(R("PR", 128 * k, 128 * k + 128), R("Dm"), float(k), eq)

    conv = lambda a, b: ts(R("Bf", a, b), R("Bs", a + a // NS * 8, b + a // NS * 8), OFF, add)
    askers(R("F0"), "Wo", [rots, lambda: (iota(R("IK", 0, 768), [[0, 768]], 0, 0), conv(0, NS))])
    cp(R("Wo", 0, 192), IND(R("Bs", 0, SP), R("Wo", 192, 204)))
    send("aW", nxt, R("sW" if last else "W0"), R("Wo"))
    for k in range(1, 8):
        act(R("SMa", 128 * (k - 1), 128 * k), R("Dm"), ACT.Abs, bias=-(16 - k) / 2.0)
    for k in range(1, 8):
        act(R("SM", 128 * (k - 1), 128 * k), R("SMa", 128 * (k - 1), 128 * k), ACT.Abs, bias=-(16 - k) / 2.0)
    act(R("SM"), R("SM"), ACT.Relu, bias=1.0, scale=-2.0)
    if first:
        act(R("Rb"), R("Rf"), CP)
        act(R("Rn"), R("Rf"), CP, scale=-1.0)
        mm(P(7, 0, 128), R("RfT"), R("tf"), True, True)
        act(R("RO"), P(7, 0, 128), ACT.Sign)
        act(R("RO"), R("RO"), ID, bias=-65536.0, scale=65536.0)
    act(CJ, PM, ID, bias=1536.0 - 1048576.0, scale=4096.0)
    act(NPM, PM, CP, scale=-1.0)
    act(CG, PM, ID, bias=-8192.0 * 1536)
    act(CT, P15, CP, scale=-1.0)
    act(CE, col("mk", 1), ID, bias=24.0, scale=12.0)
    act(R("oEf", 0, 12), R("k12", 0, 12), CP)
    act(CE, col("mk", 2), ID, bias=CE, scale=-12.0)
    act(R("IK", V, V + 1), col("mk", 0), CP, scale=-1000.0)
    act(R("oEf", 12, 24), R("k12", 0, 12), ID, bias=CE)

    def later():
        act(R("OBp"), R("OB"), CP, scale=4096.0)
        act(R("OBm"), R("OB"), CP, scale=-2048.0)
        act(R("ZCf"), R("AM"), ACT.Abs, bias=NPM)
        act(R("selK"), R("OBp"), CP, scale=col("mk", 0))
        act(R("selI"), R("OB"), CP, scale=col("mk", 1))
        act(R("ZC"), R("ZCf"), ID, bias=-393216.0, scale=8388608.0)
        act(R("AllS"), R("All1"), CP, scale=0.0625)
        for k, d in enumerate((D1, D2, D1)):
            act(R("D36", 12 * k, 12 * k + 12), R("aw"), ID, bias=float(d))

    for i in range(16):
        ts(R("BsH", 144 * i, 144 * i + 144), R("All1"), col("mk", i), mul)
    conv(NS, 2 * NS)
    conv(2 * NS, 2 * NS + 512)
    conv(2 * NS + 512, V)
    select(R("PR", 128, 1152), R("PR", 128, 1152), [[0, 8], [-1, 128]], ALU.not_equal, 0, 1, -1.0)
    select(XH, XO, [[0, 8], [-1, 16]], ALU.is_ge, 7, 0)
    iota(R("IK", 768, V), [[0, V - 768]], 0, 0)
    kv = 84 if first else 96
    act(R("C", 16 * kv, V), IND(R("Bf"), R("Mq", kv, 192)), CP)
    cp(R("C", 0, 768), IND(R("Bf"), R("Mq", 0, 48)))
    if first:
        cp(R("rf"), R("sW"))
        mm(P(7, 0, 208), R("Rf"), R("rf"), True, True)
    cp(R("C", 768, 16 * kv), IND(R("Bf"), R("Mq", 48, kv)))
    if first:
        cp(R("W0"), P(7, 0, 208))
    act(R("Xo", 0, 192), IND(R("X", 0, XW), R("Wo", 192, 204)), CP)
    send("aU", nxt, R("Xu0"), R("Xo"))
    later()
    iota(R("IK", V + 1, 3080), [[0, 3079 - V]], 0, 0)
    iota(R("rst"), [[0, 192]], int(KMAX), 0)
    select(R("rst"), R("rst"), [[0, 12], [-1, 16]], ALU.is_ge, 0, 0, -3.0e7)
    if last:
        iota(R("sB1", NS, SP), [[0, 8]], V, 0); iota(R("sB2", NS, SP), [[0, 8]], V, 0)
    send("aB1", nxt, R("Bp1"), R("sB1") if last else R("Bs", SP, 2 * SP))
    iota(R("Ev", NS, V), [[0, 2 * NS]], 0, 0)
    iota(R("one"), [[0, 192]], 1, 0)
    iota(R("Cv", 0, 192), [[0, 192]], V + int(OFF), 0)
    iota(R("LR2", 0, 192), [[0, 192]], V, 0)

    def rows():
        cp(R("blf", 0, 384), R("blk", 0, 384))
        ts(R("blt"), R("blk", 384, 576), float(V), eq, 900.0, mul)
        cp(R("oE"), R("oEf"))
        tt(R("blf", 384, 576), R("blk", 384, 576), R("blt"), add)
        dma("s", [(R("IK", 0, V, 1, 0, 128, 16), R("blf", 192, 384)), (R("IK", 0, V, 1, 1, 128, 16), R("blf", 384, 576))])
        if last:
            dma("s", [(R("Mr", 0, V, 1, 18, 128, 16), R("blf", 0, 192, 1, 0, 112)), (R("Mr", 0, V, 1, 2, 3), R("blf", 0, 192, 1, 112, 128))])
        else:
            dma("s", [(R("Mr", 0, V, 1, 2, 128, 16), R("blf", 0, 192))])

    def cross(out, src, n):
        for e in range(2):
            for h in range(2):
                mm(P(out, e, n, 2), R("LX", 128 * (2 * e + h), 128 * (2 * e + h + 1)), R(src, h, n, 2), h == 0, h == 1)

    for t in range(RO):
        W, Xu, GV = "W%d" % t, "Xu%d" % t, "GV%d" % t
        Cw, Xw = R("C", 0, 3080), R("X", 0, 3088)
        lo, hi = range(8), range(8, 16)
        vb, rb = (0, 6, 7), (1, 2, 1)
        xv = lambda ch, j: R("Xv", 1024 * ch + j, 1024 * ch + 1024, 16)
        mxs = lambda ch, j, n=1: R("MX", 1024 * ch + 64 * j, 1024 * ch + 64 * (j + n))
        part = lambda n, ch: R(n, 64 * ch, 64 * ch + 64)
        key = lambda ch: P(vb[ch], 0, 64)

        def far(a0, a1):
            ts(R("Y16", 16 * a0, 16 * a1), IND(Cw, R(W, a0, a1)), -1536.0 - OFF, add)

        def pick(ch):
            for j in range(16):
                mm(key(ch), sel("BsH", j, (j + t) % 16), R("Y16", 1024 * ch + j, 1024 * ch + 1024, 16), j == 0, j == 15)

        def cand(ch, before=None):
            ts(part("v16", ch), key(ch), 1536.0, add)
            act(R("Xv", 1024 * ch, 1024 * ch + 1024), IND(Xw, part("v16", ch)), CP)
            ts(part("Vh", ch), key(ch), 12582912.0, add, -12582912.0, add)
            if before:
                before()
            for k in range(1, 9):
                mm(P(rb[ch], 64 * k - 64, 64 * k), R("PR", 128 * k, 128 * k + 128), part("Vh", ch), True, True)

        def sup(ch):
            ts(R("EQ", 512 * ch, 512 * ch + 512), P(rb[ch], 0, 512), 0.0, eq)
            for k in range(1, 9):
                c0 = 512 * ch + 64 * k
                mm(P(3, 64 * ch, 64 * ch + 64), R("SM", 128 * (k - 1), 128 * k) if k < 8 else R("Ib"), R("EQ", c0 - 64, c0), k == 1, k == 8)

        def own():
            if t:
                act(R(Xu, 0, 192), IND(R("Xp%d" % t), R("us") if first else R(W, 192, 204)), CP)
            mm(P(5, 0, 192), XI, R(Xu, 0, 192), True, True)

        def neg(ch, js):
            for j in js:
                mm(key(ch), sel("AllN", j), xv(ch, j), j == 0, False)

        def dif(ch, js, b):
            for n, j in enumerate(js):
                mm(P(b, 64 * n, 64 * n + 64), R("Ib"), xv(ch, j), True, False)
                mm(P(b, 64 * n, 64 * n + 64), XN, part(Xu, ch), False, True)
            act(mxs(ch, js[0], 8), P(b, 0, 512), ACT.Abs, scale=0.5)

        def big(ch, js):
            for j in js:
                tt(mxs(ch, j), xv(ch, j), P(5, 64 * ch, 64 * ch + 64), mx)

        def pos(ch, js, start=False):
            for j in js:
                mm(key(ch), sel("AllP", j), mxs(ch, j), start and j == js[0], False)

        def tail(ch):
            mm(key(ch), R("Ib"), part("pen", ch), False, False)
            mm(key(ch), If, part("s2n", ch), False, False)
            mm(key(ch), R("PR", 0, 128), part("Vh", ch), False, True)
            tr(part("Tk", ch), key(ch))

        if t == 0:
            cp(R("uwf"), R(W, 192, 204))
        else:
            lr = "LR%d" % (t - 1)
        far(0, 64)
        cross(4, "uwf", 12)
        if first and t:
            mm(P(2, 0, 12), R("RfT"), R("uwf"), True, True)
        act(R("Tw", 36, 48), P(4, 0, 12), CP)
        pick(0)
        far(64, 96)
        if first and t:
            ts(R("us"), P(2, 0, 12), -float(NS * t), add)
        cand(0)
        far(96, 128)
        pick(1)
        far(128, 160)
        neg(0, range(16))
        cand(1)
        far(160, 192)
        pick(2)
        sup(0)
        own()
        cand(2, lambda: sup(1))
        neg(1, lo)
        dif(1, hi, 4)
        big(0, lo)
        sup(2)
        mm(key(0), XO, part(Xu, 0), False, False)
        mm(key(1), XH, part(Xu, 1), False, False)
        pos(0, lo)
        dif(2, lo, 2)
        act(R("s2n"), P(3, 0, 192), ID, bias=CJ, scale=-1048576.0)
        act(R("pen"), P(3, 0, 192), ACT.Relu, bias=67108864.0, scale=-67108864.0)
        dif(2, hi, 1)
        if t:
            cp(R("m16"), R(lr, 384, 408))
        big(0, hi); big(1, lo)
        if t == 0:
            rows()
            ts(R("F12"), R("Mq", 64, 192), float(V), eq)
        else:
            cp(IND(R("Mr"), R("m16", 12, 24)), R(lr, 192, 384))
            act(IND(R("Mr"), R("m16", 0, 12)), R("LR2", 0, 192), ACT.Silu)
        pos(1, hi); pos(0, hi); pos(2, lo, True); tail(0); pos(1, lo); tail(1); pos(2, hi); tail(2)
        scan(R("Sk"), R("rst"), R("Tk"), KMAX, mx, mn)
        cp(R("ki"), R("Sk", 15, 192, 16))
        ts(R("vs", 0, 12), R("ki"), 4095, ALU.bitwise_and)
        ts(R("s16"), R("ki"), 12, ALU.arith_shift_right, -16, ALU.bitwise_and)
        ts(R("vs", 12, 24), R("ki"), 16, ALU.arith_shift_right)
        ts(R("v1k"), R("vs", 0, 12), 8192.0, mul, CG, add)
        cp(R("Tw", 12, 36), R("vs"))
        tt(R("Tw", 0, 12), R("v1k"), R("s16"), add)
        cross(2, "Tw", 24)
        cp(R("E"), IND(R("Tw"), R("oE")))
        cp(R("QW"), P(2, 0, 24))
        cp(R("vw16"), P(2, 12, 24))
        tr(R(GV, 192, 576), R("E"))
        if t == RO - 1:
            send("aV", prv, R("LR2", 192, 384), R(GV, 384, 576))
        act(R("thr"), R("QW", 0, 12), ID, bias=CT)
        act(R("nhi"), R("QW", 12, 24), ID, bias=8192.0 * 1536 - 4000.0, scale=-8192.0)
        act(R(GV, 0, 192), R(GV, 192, 384), ID, bias=16.0)
        act(R("IKg"), IND(R("IK", 0, 3080), R("vw16")), CP)
        Z = P(3, 0, 192)
        mm(Z, R("Ib"), R("ZC"), True, False)
        tt(R("eqd"), IND(R("QW"), R("oE", 0, 12)), R(GV, 192, 384), ALU.is_lt)
        tt(R("rej"), IND(R("IK", 0, 3080), R("vw16")), R(GV, 384, 576), ALU.is_le)
        mm(Z, R("OBp"), R("eqd"), False, False)
        mm(Z, R("selK"), R("rej"), False, False)
        mm(Z, R("selI"), R("IKg"), False, False)
        for c in range(12):
            c0 = 192 * c
            ts(R("C1", c0, c0 + 176), R(GV, 16 * c + 16, 16 * c + 192), col("thr", c), ALU.is_gt)
            act(R("C2", c0, c0 + 192), R(GV, 192, 384), ACT.Sign, bias=col("nhi", c))
            if c < 11:
                mm(P(3, 16 * c + 16, 192), R("OBp"), R("C1", c0, c0 + 176 - 16 * c), False, False)
            if c:
                mm(P(3, 0, 16 * c), R("OBp"), R("C1", c0 + 176 - 16 * c, c0 + 176), False, False)
            mm(Z, R("OBm"), R("C2", c0, c0 + 192), False, c == 11)
        if t < RO - 1:
            act(R("Xv3"), IND(Xw, R("vw16")), CP, scale=3.0)
            mm(P(7, 0, 192), R("Ib"), R("Xv3"), True, False)
            mm(P(7, 0, 192), XI, R(Xu, 0, 192), False, True)
            act(R("Cv", 192, 384), IND(R("Bf"), R("vw16")), CP)
            act(R("xr"), P(7, 0, 192), ID, bias=191.625, scale=0.25)
            act(R("xn"), R("xr"), ID, bias=-192.0)
        scan(R("SZ"), R("rst"), Z, KMAX, mx, mn)
        Zw = R("SZ", 15, 192, 16)
        tt(R(GV, 576, 588), Zw, R("D36", 0, 12), mn)
        ts(R("L"), Zw, 4096.0, ALU.is_ge, 8192.0, mul)
        if t < RO - 1:
            cp(R("o16", 0, 12), R(GV, 576, 588))
            tt(R("TT", 0, 12), R("uwf"), R("L"), add)
            cp(IND(R("Ev"), R("o16", 0, 12)), R("one"))
            act(IND(R("C"), R("o16", 0, 12)), R("Cv", 0, 192), ACT.Silu)
            s0 = NS * (t + 1)
            mm(P(2, 0, 64), R("Ib"), R("F12", 64 * t, 64 * t + 64), True, False)
            for q in range(16):
                mm(P(2, 0, 64), sel("AllS", q), R("Ev", s0 + q, s0 + NS, 16), False, q == 15)
        else:
            tt(R("TT", 0, 12), R("uwf"), R("L"), add)
        tt(R("TT", 12, 24), R("QW", 12, 24), R("L"), add)
        tt(R(GV, 588, 612), R("TT"), R("D36", 12, 36), mn)
        c0 = 192 if t == RO - 1 else 0
        send("aL%d" % t, prv, R("LR%d" % t, 192 + c0, 408), R(GV, 384 + c0, 600))
        cp(R("o16", 12, 36), R(GV, 588, 612))
        keys = lambda: cp(IND(R("IK"), R("o16", 24, 36)), R(GV, 384, 576))
        if t < RO - 1:
            def feats():
                cp(IND(R("X"), R("o16", 24, 36)), R("xn"))
                send("aX%d" % (t + 1), nxt, R("Xp%d" % (t + 1)), R("X", s0, s0 + XW))
                if t == 0:
                    send("aB2", nxt, R("Bp2"), R("sB2") if last else R("Bs", 2 * SP, 3 * SP))

            def tables():
                act(IND(R("C"), R("o16", 12, 24)), R("Cv", 192, 384), ACT.Silu)
                keys()
            Wn = "W%d" % (t + 1)
            askers(P(2, 0, 64), Wn, [feats, tables])
            ts(R("uwf"), P(6, 0, 12), 512.0 + s0, add)
            cp(R(Wn, 0, 192), IND(R("Bp%d" % (t + 1)), R(Wn, 192, 204)))
        else:
            keys()
            dma("s", [(T.yk[:, :], R("IK", 0, V, 1, 0, 128, 16))])
            cp(R("m16"), R("LR2", 384, 408))
            cp(IND(R("Mr"), R("m16")), R("LR2", 0, 384))
            if last:
                dma("a", [(T.ym[0:7, :], R("Mr", 0, V, 1, 18, 128, 16)), (T.ym[7:8, :], R("Mr", 0, V, 1, 2, 3))])
            else:
                dma("a", [(T.ym[:, :], R("Mr", 0, V, 1, 2, 128, 16))])
    for s in sorted(totals):
        wait("s", s, totals[s], {})
